import numpy as np
import ml_dtypes


def mxq(x, axis, fmt="e4m3"):
    dtype, down = {"e4m3": (ml_dtypes.float8_e4m3fn, 7), "e5m2": (ml_dtypes.float8_e5m2, 14)}[fmt]
    v = np.moveaxis(np.asarray(x, np.float32).astype(ml_dtypes.bfloat16).astype(np.float64), axis, -1)
    blocks = v.reshape(v.shape[:-1] + (-1, 32))
    amax = np.abs(blocks).max(-1, keepdims=True)
    byte = np.maximum(np.where(amax > 0, np.frexp(amax)[1] - 1 + 127, 0) - down, 1)
    scale = np.exp2(byte - 127.0)
    codes = (blocks / scale).astype(np.float32).astype(dtype).astype(np.float64)
    return np.moveaxis((codes * scale).reshape(v.shape), -1, axis)


WIDE = False


def mx_kscale(k):
    if not WIDE:
        return np.ones(k)
    levels = np.array([10, -10, 5, -5, 0])
    if k % 512:
        return np.exp2(np.random.permutation(np.resize(levels, k // 32))).repeat(32)
    a = np.empty((k // 512, 16))
    for p in range(k // 512):
        a[p, :8] = np.random.permutation(np.resize(levels, 8))
        for g in range(8):
            far = levels[np.abs(levels - a[p, g]) >= 10]
            a[p, g + 8] = far[np.random.randint(len(far))]
    return np.exp2(a.ravel()).repeat(32)


def f64(x):
    return np.asarray(x).astype(np.float64)


def striped(idx):
    return np.tile(idx.reshape(-1, 16).T, (8, 1)).astype(np.uint16)


def unstriped(offs):
    return offs[:16].T.reshape(-1).astype(np.int64)


def pack_weight(w):
    k, n = w.shape
    w = f64(np.asarray(w, np.float32).astype(ml_dtypes.bfloat16)).reshape(k // 32, 32, n)
    amax = np.abs(w).max(1)
    byte = np.clip(np.where(amax > 0, np.frexp(amax)[1] - 1 + 127 - 7, 1), 1, 254)
    scaled = (w * np.exp2(127.0 - byte)[:, None, :]).reshape(k, n).astype(np.float32)
    words = np.ascontiguousarray(scaled.reshape(k // 512, 128, 4, n).transpose(0, 1, 3, 2)).astype(ml_dtypes.float8_e4m3fn).view(np.uint8)
    return words, np.ascontiguousarray(byte.astype(np.uint8).reshape(k // 512, 16, n))


def unpack_weight(words, scales):
    g, p, n, _ = words.shape
    vals = np.ascontiguousarray(words).view(ml_dtypes.float8_e4m3fn).astype(np.float64) * np.repeat(np.exp2(scales.astype(np.float64) - 127.0), 8, axis=1)[..., None]
    return vals.transpose(0, 1, 3, 2).reshape(g * 512, n)


E2M1 = np.array([0.0, 0.5, 1.0, 1.5, 2.0, 3.0, 4.0, 6.0, -0.0, -0.5, -1.0, -1.5, -2.0, -3.0, -4.0, -6.0])


def pack_fp4(w):
    k, n = w.shape
    w = f64(np.asarray(w, np.float32).astype(ml_dtypes.bfloat16)).reshape(k // 32, 32, n)
    amax = np.abs(w).max(1)
    mant, ex = np.frexp(amax / 6.0)
    byte = np.clip(np.where(amax > 0, np.where(mant > 0.5, ex, ex - 1) + 127, 1), 1, 254)
    scaled = (w * np.exp2(127.0 - byte)[:, None, :]).reshape(k, n).astype(np.float32)
    c = np.ascontiguousarray(scaled.reshape(k // 512, 128, 4, n).transpose(0, 1, 3, 2)).astype(ml_dtypes.float4_e2m1fn).view(np.uint8) & 0xF
    words = (c[..., 0::2] | (c[..., 1::2] << 4)).reshape(k // 512, 128, 2 * n)
    return np.ascontiguousarray(words), np.ascontiguousarray(byte.astype(np.uint8).reshape(k // 512, 16, n))


def unpack_fp4(words, scales):
    g, _, n = scales.shape
    words = np.ascontiguousarray(words).reshape(g, 128, n, 2)
    nib = np.empty((g, 128, n, 4), np.uint8)
    nib[..., 0::2] = words & 0xF
    nib[..., 1::2] = words >> 4
    vals = E2M1[nib] * np.repeat(np.exp2(scales.astype(np.float64) - 127.0), 8, axis=1)[..., None]
    return vals.transpose(0, 1, 3, 2).reshape(g * 512, n)


def planes(y):
    n, m = y.shape
    v = y.astype(np.float32).astype(ml_dtypes.bfloat16).astype(np.float64).reshape(n // 32, 32, m)
    top = np.abs(v).max(1)
    byte = np.clip(np.where(top > 0, np.frexp(top)[1] - 1 + 127 - 7, 1), 1, 254)
    codes = (v * np.exp2(127.0 - byte)[:, None, :]).reshape(n, m).astype(np.float32).astype(ml_dtypes.float8_e4m3fn).view(np.uint8)
    words = codes.reshape(n // 512, 128, 4, m).transpose(0, 1, 3, 2)
    return np.ascontiguousarray(words), np.ascontiguousarray(byte.astype(np.uint8).reshape(n // 512, 16, m))


def silu(v):
    return v / (1.0 + np.exp(-np.maximum(v, -700.0)))


K, T, S, W, H, N = 512, 1024, 512, 1024, 512, 512


def setup_inputs():
    n = np.random.standard_normal
    s = mx_kscale(K)[:, None]
    u = mx_kscale(H)
    packed_xT = pack_weight(n((K, T)) * s)
    packed_eT = pack_weight(n((K, W)) * s)
    packed_w3 = pack_fp4(n((H, N)) / np.sqrt(H) / u[:, None])
    return {
        "x_words": packed_xT[0],
        "x_scales": packed_xT[1],
        "e_words": packed_eT[0],
        "e_scales": packed_eT[1],
        "w1": (n((K, H)) / np.sqrt(2 * K) / s * u).astype(np.float32),
        "w2": (n((K, H)) / np.sqrt(2 * K) / s * u).astype(np.float32),
        "w3_words": packed_w3[0],
        "w3_scales": packed_w3[1],
        "skip": (n((N, S))).astype(np.float32),
        "offs": striped(np.random.permutation(T)[:S]),
        "tok": striped(np.random.permutation(W)[:S]),
    }


def reference(x_words, x_scales, e_words, e_scales, w1, w2, w3_words, w3_scales, skip, offs, tok):
    xq = unpack_weight(x_words, x_scales)[:, unstriped(offs)]
    e_tok = unpack_weight(e_words, e_scales)[:, unstriped(tok)]
    h = silu(mxq(f64(w1), 0, "e4m3").T @ xq + mxq(f64(w2), 0, "e4m3").T @ e_tok)
    y = unpack_fp4(w3_words, w3_scales).T @ mxq(h, 0, "e4m3")
    out_0 = y + f64(skip)
    return (out_0,) + planes(out_0)

@@ -1,0 +1,225 @@
+from contextlib import ExitStack
+
+import concourse.mybir as mybir
+
+K, T, S, H, N = 512, 1024, 512, 512, 512
+FLOPS = 2 * S * (2 * K * H + H * N)
+
+F32 = mybir.dt.float32
+BF16 = mybir.dt.bfloat16
+I32 = mybir.dt.int32
+U32 = mybir.dt.uint32
+U16 = mybir.dt.uint16
+U8 = mybir.dt.uint8
+FP8X4 = mybir.dt.float8_e4m3fn_x4
+FP4X4 = mybir.dt.float4_e2m1fn_x4
+SILU = mybir.ActivationFunctionType.Silu
+ADD = mybir.AluOpType.add
+
+P = 128
+PACK = 4
+CHUNK = 128
+CHUNKS = S // CHUNK
+LIST_COLS = CHUNK // 16
+HALF = H // 2
+
+
+def tile_picked_zeagle_silu_po_kernel(
+    tc, x_words, x_scales, e_words, e_scales, w1, w2, w3_words, w3_scales, skip, offs, tok,
+    out_0, out_1, out_2,
+):
+    nc = tc.nc
+    with ExitStack() as ctx:
+        keep = ctx.enter_context(tc.tile_pool(name="keep", bufs=1))
+        psum = ctx.enter_context(tc.psum_pool(name="psum", bufs=1))
+
+        def tile(shape, dtype, name):
+            return keep.tile(shape, dtype, name=name, align_bytes=64)
+
+        def load_scale_rows(queue, plane, rows):
+            for q in range(4):
+                queue.dma_start(
+                    out=plane[32 * q : 32 * q + 4, :].bitcast(I32),
+                    in_=rows[0, 4 * q : 4 * q + 4, :].bitcast(I32),
+                )
+
+        def load_weight_half(w, half, name):
+            raw = tile([P, PACK, HALF], F32, name)
+            cols = slice(half * HALF, (half + 1) * HALF)
+            nc.sync.dma_start(out=raw[:], in_=w[:, cols].rearrange("(p j) c -> p j c", j=PACK))
+            return raw
+
+        def load_words(words, name):
+            table = tile([P, T], I32, name)
+            nc.sync.dma_start(out=table[:], in_=words[0].rearrange("p c r -> p (c r)").bitcast(I32))
+            return table
+
+        offs_sb = keep.tile([P, S // 16], U16, name="offs_sb")
+        tok_sb = keep.tile([P, S // 16], U16, name="tok_sb")
+        xs_table = tile([P, T], U8, "xs_table")
+        es_table = tile([P, T], U8, "es_table")
+        w3s_raw = tile([P, N], U8, "w3s_raw")
+        warm = tile([P, 16], F32, "warm")
+        warm_out = tile([P, 16], F32, "warm_out")
+
+        nc.vector.memset(xs_table[:].bitcast(I32), 0)
+        nc.gpsimd.memset(es_table[:].bitcast(I32), 0)
+        nc.vector.memset(warm[:], 0.0)
+        nc.gpsimd.memset(w3s_raw[:].bitcast(I32), 0)
+
+        w1_raw = [None, None]
+        w2_raw = [None, None]
+        nc.sync.dma_start(offs_sb[:], offs)
+        nc.sync.dma_start(tok_sb[:], tok)
+        w1_raw[0] = load_weight_half(w1, 0, "w1_raw0")
+        w1_raw[1] = load_weight_half(w1, 1, "w1_raw1")
+        load_scale_rows(nc.scalar, xs_table, x_scales)
+        nc.scalar.activation(out=warm_out[:], in_=warm[:], func=SILU)
+        xw_table = load_words(x_words, "xw_table")
+        w2_raw[0] = load_weight_half(w2, 0, "w2_raw0")
+        load_scale_rows(nc.sync, es_table, e_scales)
+        w2_raw[1] = load_weight_half(w2, 1, "w2_raw1")
+        ew_table = load_words(e_words, "ew_table")
+        w3w_raw = tile([P, 2 * N], U8, "w3w_raw")
+        nc.sync.dma_start(out=w3w_raw[:].bitcast(I32), in_=w3_words[0].bitcast(I32))
+        load_scale_rows(nc.sync, w3s_raw, w3_scales)
+        skip_sb = []
+        for half in range(2):
+            part = tile([P, PACK, S // 2], F32, "skip%d" % half)
+            cols = slice(half * S // 2, (half + 1) * S // 2)
+            nc.sync.dma_start(out=part[:], in_=skip[:, cols].rearrange("(p t) j -> p t j", t=PACK))
+            skip_sb.append(part)
+
+        def round_and_deal(grouped, raw, half):
+            m_half = slice(half * HALF // PACK, (half + 1) * HALF // PACK)
+            nc.scalar.copy(
+                out=grouped[:, :, m_half, :].rearrange("p t m j -> p m j t"),
+                in_=raw[:].rearrange("p j (m t) -> p m j t", t=PACK),
+            )
+
+        xs_picked = tile([P, S], U8, "xs_picked")
+        es_picked = tile([P, S], U8, "es_picked")
+        xw_picked = tile([P, S], U32, "xw_picked")
+        ew_picked = tile([P, S], U32, "ew_picked")
+        w1_grouped = tile([P, PACK, P, PACK], BF16, "w1_grouped")
+        w2_grouped = tile([P, PACK, P, PACK], BF16, "w2_grouped")
+        w1_codes = tile([P, H], U32, "w1_codes")
+        w2_codes = tile([P, H], U32, "w2_codes")
+        w1_plane = tile([P, H], U8, "w1_plane")
+        w2_plane = tile([P, H], U8, "w2_plane")
+        w3_codes = tile([P, PACK, P, 2], U8, "w3_codes")
+        w3_plane = tile([P, PACK, P], U8, "w3_plane")
+
+        for half in range(2):
+            round_and_deal(w1_grouped, w1_raw[half], half)
+        nc.vector.tensor_copy(xs_picked[:], xs_table[:].indirect(offs_sb[:]))
+        nc.vector.tensor_copy(xw_picked[:], xw_table[:].bitcast(U32).indirect(offs_sb[:]))
+        nc.vector.quantize_mx(
+            out=w1_codes[:].bitcast(FP8X4), scales=w1_plane[:],
+            in_=w1_grouped[:].rearrange("p t m j -> p (t m j)"),
+        )
+        nc.vector.tensor_copy(es_picked[:], es_table[:].indirect(tok_sb[:]))
+        for half in range(2):
+            round_and_deal(w2_grouped, w2_raw[half], half)
+        for t in range(PACK):
+            cols = slice(t * P, (t + 1) * P)
+            nc.vector.quantize_mx(
+                out=w2_codes[:, cols].bitcast(FP8X4), scales=w2_plane[:, cols],
+                in_=w2_grouped[:, t, :, :].rearrange("p m j -> p (m j)"),
+            )
+
+        def gather_e(c):
+            cols = slice(c * CHUNK, (c + 1) * CHUNK)
+            entries = tok_sb[:, c * LIST_COLS : (c + 1) * LIST_COLS]
+            nc.vector.tensor_copy(ew_picked[:, cols], ew_table[:].bitcast(U32).indirect(entries))
+
+        h_codes = tile([P, S], U32, "h_codes")
+        h_plane = tile([P, S], U8, "h_plane")
+        y_codes = tile([P, S], U32, "y_codes")
+        y_plane = tile([P, S], U8, "y_plane")
+        h_bf = [tile([P, CHUNK, PACK], BF16, "h_bf%d" % c) for c in range(CHUNKS)]
+        y_bf = [tile([P, CHUNK, PACK], BF16, "y_bf%d" % c) for c in range(CHUNKS)]
+        y_f32 = [tile([P, PACK, CHUNK], F32, "y_f32%d" % c) for c in range(CHUNKS)]
+
+        def first_layer(c):
+            cols = slice(c * CHUNK, (c + 1) * CHUNK)
+            bank = psum.tile([P, PACK, CHUNK], F32, name="pre%d" % c)
+            for t in range(PACK):
+                wc = slice(t * P, (t + 1) * P)
+                nc.tensor.matmul_mx(
+                    out=bank[:, t, :], lhsT=w1_codes[:, wc].bitcast(FP8X4), lhsT_scale=w1_plane[:, wc],
+                    rhs=xw_picked[:, cols].bitcast(FP8X4), rhs_scale=xs_picked[:, cols],
+                    start=True, stop=False,
+                )
+                nc.tensor.matmul_mx(
+                    out=bank[:, t, :], lhsT=w2_codes[:, wc].bitcast(FP8X4), lhsT_scale=w2_plane[:, wc],
+                    rhs=ew_picked[:, cols].bitcast(FP8X4), rhs_scale=es_picked[:, cols],
+                    start=False, stop=True,
+                )
+            nc.scalar.activation(out=h_bf[c][:], in_=bank[:].rearrange("p t n -> p n t"), func=SILU)
+
+        def second_layer(c):
+            cols = slice(c * CHUNK, (c + 1) * CHUNK)
+            nc.vector.quantize_mx(
+                out=h_codes[:, cols].bitcast(FP8X4), scales=h_plane[:, cols],
+                in_=h_bf[c][:].rearrange("p n t -> p (n t)"),
+            )
+            bank = psum.tile([P, PACK, CHUNK], F32, name="post%d" % c)
+            for t in range(PACK):
+                nc.tensor.matmul_mx(
+                    out=bank[:, t, :],
+                    lhsT=w3_codes[:, t, :, :].rearrange("p m b -> p (m b)").bitcast(FP4X4),
+                    lhsT_scale=w3_plane[:, t, :],
+                    rhs=h_codes[:, cols].bitcast(FP8X4), rhs_scale=h_plane[:, cols],
+                    start=True, stop=True,
+                )
+            return bank
+
+        def add_and_store(c, bank):
+            cols = slice(c * CHUNK, (c + 1) * CHUNK)
+            in_half = slice((c % 2) * CHUNK, (c % 2 + 1) * CHUNK)
+            nc.vector.tensor_tensor(y_f32[c][:], bank[:], skip_sb[c // 2][:, :, in_half], ADD)
+            nc.sync.dma_start(out=out_0[:, cols].rearrange("(p t) j -> p t j", t=PACK), in_=y_f32[c][:])
+            nc.scalar.copy(
+                out=y_bf[c][:].rearrange("p (g i) t -> p g t i", i=4),
+                in_=y_f32[c][:].rearrange("p t (g i) -> p g t i", i=4),
+            )
+
+        def quantise_out(c):
+            cols = slice(c * CHUNK, (c + 1) * CHUNK)
+            nc.vector.quantize_mx(
+                out=y_codes[:, cols].bitcast(FP8X4), scales=y_plane[:, cols],
+                in_=y_bf[c][:].rearrange("p n t -> p (n t)"),
+            )
+            words = out_1[0].rearrange("p c r -> p (c r)").bitcast(I32)
+            nc.sync.dma_start(out=words[:, cols], in_=y_codes[:, cols].bitcast(I32))
+
+        gather_e(0)
+        first_layer(0)
+        gather_e(1)
+        first_layer(1)
+        nc.vector.tensor_copy(
+            w3_codes[:].rearrange("p t m b -> p m t b"),
+            w3w_raw[:].rearrange("p (m t b) -> p m t b", t=PACK, b=2),
+        )
+        nc.vector.tensor_copy(
+            w3_plane[:].rearrange("p t m -> p m t"),
+            w3s_raw[:].rearrange("p (m t) -> p m t", t=PACK),
+        )
+        banks = {}
+        for step in range(CHUNKS + 2):
+            if step < CHUNKS:
+                banks[step] = second_layer(step)
+            if step + 2 < CHUNKS:
+                gather_e(step + 2)
+                first_layer(step + 2)
+            if 0 <= step - 2 < CHUNKS:
+                quantise_out(step - 2)
+            if 0 <= step - 1 < CHUNKS:
+                add_and_store(step - 1, banks[step - 1])
+        for q in range(4):
+            queue = nc.scalar if q % 2 else nc.sync
+            queue.dma_start(
+                out=out_2[0, 4 * q : 4 * q + 4, :].bitcast(I32),
+                in_=y_plane[32 * q : 32 * q + 4, :].bitcast(I32),
+            )

@@ -33,8 +33,8 @@ def tile_picked_zeagle_silu_po_kernel(
         keep = ctx.enter_context(tc.tile_pool(name="keep", bufs=1))
         psum = ctx.enter_context(tc.psum_pool(name="psum", bufs=1))
 
-        def tile(shape, dtype, name):
-            return keep.tile(shape, dtype, name=name, align_bytes=64)
+        def tile(shape, dtype, name, tag=None):
+            return keep.tile(shape, dtype, name=name, tag=tag or name, align_bytes=64)
 
         def load_scale_rows(queue, plane, rows):
             for q in range(4):
@@ -59,48 +59,45 @@ def tile_picked_zeagle_silu_po_kernel(
         xs_table = tile([P, T], U8, "xs_table")
         es_table = tile([P, T], U8, "es_table")
         w3s_raw = tile([P, N], U8, "w3s_raw")
+
         warm = tile([P, 16], F32, "warm")
         warm_out = tile([P, 16], F32, "warm_out")
-
-        nc.vector.memset(xs_table[:].bitcast(I32), 0)
+        nc.gpsimd.memset(xs_table[:].bitcast(I32), 0)
         nc.gpsimd.memset(es_table[:].bitcast(I32), 0)
-        nc.vector.memset(warm[:], 0.0)
         nc.gpsimd.memset(w3s_raw[:].bitcast(I32), 0)
-
+        nc.vector.memset(warm[:], 0.0)
+        nc.scalar.activation(out=warm_out[:], in_=warm[:], func=SILU)
         w1_raw = [None, None]
         w2_raw = [None, None]
+        w3w_raw = tile([P, 2 * N], U8, "w3w_raw")
+        nc.sync.dma_start(out=w3w_raw[:].bitcast(I32), in_=w3_words[0].bitcast(I32))
         nc.sync.dma_start(offs_sb[:], offs)
-        nc.sync.dma_start(tok_sb[:], tok)
-        w1_raw[0] = load_weight_half(w1, 0, "w1_raw0")
-        w1_raw[1] = load_weight_half(w1, 1, "w1_raw1")
-        load_scale_rows(nc.scalar, xs_table, x_scales)
-        nc.scalar.activation(out=warm_out[:], in_=warm[:], func=SILU)
         xw_table = load_words(x_words, "xw_table")
+        load_scale_rows(nc.sync, xs_table, x_scales)
+        w1_raw[0] = load_weight_half(w1, 0, "w1_raw0")
+        nc.sync.dma_start(tok_sb[:], tok)
+        w1_raw[1] = load_weight_half(w1, 1, "w1_raw1")
         w2_raw[0] = load_weight_half(w2, 0, "w2_raw0")
         load_scale_rows(nc.sync, es_table, e_scales)
         w2_raw[1] = load_weight_half(w2, 1, "w2_raw1")
         ew_table = load_words(e_words, "ew_table")
-        w3w_raw = tile([P, 2 * N], U8, "w3w_raw")
-        nc.sync.dma_start(out=w3w_raw[:].bitcast(I32), in_=w3_words[0].bitcast(I32))
         load_scale_rows(nc.sync, w3s_raw, w3_scales)
         skip_sb = []
-        for half in range(2):
-            part = tile([P, PACK, S // 2], F32, "skip%d" % half)
-            cols = slice(half * S // 2, (half + 1) * S // 2)
+        for piece, cols in enumerate((slice(0, CHUNK), slice(CHUNK, 2 * CHUNK), slice(2 * CHUNK, S))):
+            part = tile([P, PACK, cols.stop - cols.start], F32, "skip%d" % piece)
             nc.sync.dma_start(out=part[:], in_=skip[:, cols].rearrange("(p t) j -> p t j", t=PACK))
             skip_sb.append(part)
 
-        def round_and_deal(grouped, raw, half):
-            m_half = slice(half * HALF // PACK, (half + 1) * HALF // PACK)
-            nc.scalar.copy(
-                out=grouped[:, :, m_half, :].rearrange("p t m j -> p m j t"),
-                in_=raw[:].rearrange("p j (m t) -> p m j t", t=PACK),
+        def round_and_deal(copy, grouped, raw, half, first, last):
+            m0 = half * HALF // PACK
+            copy(
+                out=grouped[:, :, m0 + first : m0 + last, :].rearrange("p t m j -> p m j t"),
+                in_=raw[:].rearrange("p j (m t) -> p m j t", t=PACK)[:, first:last, :, :],
             )
 
         xs_picked = tile([P, S], U8, "xs_picked")
         es_picked = tile([P, S], U8, "es_picked")
         xw_picked = tile([P, S], U32, "xw_picked")
-        ew_picked = tile([P, S], U32, "ew_picked")
         w1_grouped = tile([P, PACK, P, PACK], BF16, "w1_grouped")
         w2_grouped = tile([P, PACK, P, PACK], BF16, "w2_grouped")
         w1_codes = tile([P, H], U32, "w1_codes")
@@ -110,30 +107,44 @@ def tile_picked_zeagle_silu_po_kernel(
         w3_codes = tile([P, PACK, P, 2], U8, "w3_codes")
         w3_plane = tile([P, PACK, P], U8, "w3_plane")
 
-        for half in range(2):
-            round_and_deal(w1_grouped, w1_raw[half], half)
-        nc.vector.tensor_copy(xs_picked[:], xs_table[:].indirect(offs_sb[:]))
+        nc.vector.tensor_copy(
+            w3_codes[:].rearrange("p t m b -> p m t b"),
+            w3w_raw[:].rearrange("p (m t b) -> p m t b", t=PACK, b=2),
+        )
+        round_and_deal(nc.scalar.copy, w1_grouped, w1_raw[0], 0, 0, 64)
         nc.vector.tensor_copy(xw_picked[:], xw_table[:].bitcast(U32).indirect(offs_sb[:]))
+        nc.vector.tensor_copy(xs_picked[:], xs_table[:].indirect(offs_sb[:]))
+        round_and_deal(nc.vector.tensor_copy, w1_grouped, w1_raw[1], 1, 0, 64)
         nc.vector.quantize_mx(
             out=w1_codes[:].bitcast(FP8X4), scales=w1_plane[:],
             in_=w1_grouped[:].rearrange("p t m j -> p (t m j)"),
         )
+        warm_bank = psum.tile([P, S], F32, name="warm_bank")
+        for t in range(3):
+            wc = slice(t * P, (t + 1) * P)
+            nc.tensor.matmul_mx(
+                out=warm_bank[:], lhsT=w1_codes[:, wc].bitcast(FP8X4), lhsT_scale=w1_plane[:, wc],
+                rhs=xw_picked[:].bitcast(FP8X4), rhs_scale=xs_picked[:], start=True, stop=True,
+            )
         nc.vector.tensor_copy(es_picked[:], es_table[:].indirect(tok_sb[:]))
-        for half in range(2):
-            round_and_deal(w2_grouped, w2_raw[half], half)
-        for t in range(PACK):
-            cols = slice(t * P, (t + 1) * P)
+        round_and_deal(nc.scalar.copy, w2_grouped, w2_raw[0], 0, 0, 64)
+        round_and_deal(nc.scalar.copy, w2_grouped, w2_raw[1], 1, 0, 40)
+        round_and_deal(nc.vector.tensor_copy, w2_grouped, w2_raw[1], 1, 40, 64)
+
+        def quantise_w2(pair):
+            cols = slice(pair * 2 * P, (pair + 1) * 2 * P)
             nc.vector.quantize_mx(
                 out=w2_codes[:, cols].bitcast(FP8X4), scales=w2_plane[:, cols],
-                in_=w2_grouped[:, t, :, :].rearrange("p m j -> p (m j)"),
+                in_=w2_grouped[:, 2 * pair : 2 * pair + 2, :, :].rearrange("p t m j -> p (t m j)"),
             )
 
-        def gather_e(c):
-            cols = slice(c * CHUNK, (c + 1) * CHUNK)
-            entries = tok_sb[:, c * LIST_COLS : (c + 1) * LIST_COLS]
-            nc.vector.tensor_copy(ew_picked[:, cols], ew_table[:].bitcast(U32).indirect(entries))
+        ew_first = tile([P, CHUNK], U32, "ew_first")
+        ew_picked = [ew_first[:]]
 
-        h_codes = tile([P, S], U32, "h_codes")
+        def gather_e(c):
+            entries = tok_sb[:, c * LIST_COLS : (c + 1) * LIST_COLS]
+            nc.vector.tensor_copy(ew_picked[c], ew_table[:].bitcast(U32).indirect(entries))
+
         h_plane = tile([P, S], U8, "h_plane")
         y_codes = tile([P, S], U32, "y_codes")
         y_plane = tile([P, S], U8, "y_plane")
@@ -143,7 +154,7 @@ def tile_picked_zeagle_silu_po_kernel(
 
         def first_layer(c):
             cols = slice(c * CHUNK, (c + 1) * CHUNK)
-            bank = psum.tile([P, PACK, CHUNK], F32, name="pre%d" % c)
+            bank = psum.tile([P, PACK, CHUNK], F32, name="pre%d" % (c % 2))
             for t in range(PACK):
                 wc = slice(t * P, (t + 1) * P)
                 nc.tensor.matmul_mx(
@@ -153,15 +164,16 @@ def tile_picked_zeagle_silu_po_kernel(
                 )
                 nc.tensor.matmul_mx(
                     out=bank[:, t, :], lhsT=w2_codes[:, wc].bitcast(FP8X4), lhsT_scale=w2_plane[:, wc],
-                    rhs=ew_picked[:, cols].bitcast(FP8X4), rhs_scale=es_picked[:, cols],
+                    rhs=ew_picked[c].bitcast(FP8X4), rhs_scale=es_picked[:, cols],
                     start=False, stop=True,
                 )
             nc.scalar.activation(out=h_bf[c][:], in_=bank[:].rearrange("p t n -> p n t"), func=SILU)
 
         def second_layer(c):
             cols = slice(c * CHUNK, (c + 1) * CHUNK)
+            h_codes = tile([P, CHUNK], U32, "h_codes%d" % c, tag="skip%d" % (c - 2) if c >= 2 else None)
             nc.vector.quantize_mx(
-                out=h_codes[:, cols].bitcast(FP8X4), scales=h_plane[:, cols],
+                out=h_codes[:].bitcast(FP8X4), scales=h_plane[:, cols],
                 in_=h_bf[c][:].rearrange("p n t -> p (n t)"),
             )
             bank = psum.tile([P, PACK, CHUNK], F32, name="post%d" % c)
@@ -170,17 +182,18 @@ def tile_picked_zeagle_silu_po_kernel(
                     out=bank[:, t, :],
                     lhsT=w3_codes[:, t, :, :].rearrange("p m b -> p (m b)").bitcast(FP4X4),
                     lhsT_scale=w3_plane[:, t, :],
-                    rhs=h_codes[:, cols].bitcast(FP8X4), rhs_scale=h_plane[:, cols],
+                    rhs=h_codes[:].bitcast(FP8X4), rhs_scale=h_plane[:, cols],
                     start=True, stop=True,
                 )
             return bank
 
         def add_and_store(c, bank):
             cols = slice(c * CHUNK, (c + 1) * CHUNK)
-            in_half = slice((c % 2) * CHUNK, (c % 2 + 1) * CHUNK)
-            nc.vector.tensor_tensor(y_f32[c][:], bank[:], skip_sb[c // 2][:, :, in_half], ADD)
+            added = skip_sb[c][:] if c < 2 else skip_sb[2][:, :, (c - 2) * CHUNK : (c - 1) * CHUNK]
+            nc.vector.tensor_tensor(y_f32[c][:], bank[:], added, ADD)
             nc.sync.dma_start(out=out_0[:, cols].rearrange("(p t) j -> p t j", t=PACK), in_=y_f32[c][:])
-            nc.scalar.copy(
+            copy = nc.vector.tensor_copy if c == CHUNKS - 1 else nc.scalar.copy
+            copy(
                 out=y_bf[c][:].rearrange("p (g i) t -> p g t i", i=4),
                 in_=y_f32[c][:].rearrange("p t (g i) -> p g t i", i=4),
             )
@@ -194,24 +207,25 @@ def tile_picked_zeagle_silu_po_kernel(
             words = out_1[0].rearrange("p c r -> p (c r)").bitcast(I32)
             nc.sync.dma_start(out=words[:, cols], in_=y_codes[:, cols].bitcast(I32))
 
+        quantise_w2(0)
         gather_e(0)
+        quantise_w2(1)
+        ew_rest = tile([P, S - CHUNK], U32, "ew_rest", tag="w2_grouped")
+        ew_picked.extend(ew_rest[:, c * CHUNK : (c + 1) * CHUNK] for c in range(CHUNKS - 1))
         first_layer(0)
         gather_e(1)
         first_layer(1)
-        nc.vector.tensor_copy(
-            w3_codes[:].rearrange("p t m b -> p m t b"),
-            w3w_raw[:].rearrange("p (m t b) -> p m t b", t=PACK, b=2),
-        )
+        gather_e(2)
         nc.vector.tensor_copy(
             w3_plane[:].rearrange("p t m -> p m t"),
             w3s_raw[:].rearrange("p (m t) -> p m t", t=PACK),
         )
+        gather_e(3)
         banks = {}
         for step in range(CHUNKS + 2):
             if step < CHUNKS:
                 banks[step] = second_layer(step)
             if step + 2 < CHUNKS:
-                gather_e(step + 2)
                 first_layer(step + 2)
             if 0 <= step - 2 < CHUNKS:
                 quantise_out(step - 2)

@@ -60,30 +60,25 @@ def tile_picked_zeagle_silu_po_kernel(
         es_table = tile([P, T], U8, "es_table")
         w3s_raw = tile([P, N], U8, "w3s_raw")
 
-        warm = tile([P, 16], F32, "warm")
-        warm_out = tile([P, 16], F32, "warm_out")
         nc.gpsimd.memset(xs_table[:].bitcast(I32), 0)
         nc.gpsimd.memset(es_table[:].bitcast(I32), 0)
         nc.gpsimd.memset(w3s_raw[:].bitcast(I32), 0)
-        nc.vector.memset(warm[:], 0.0)
-        nc.scalar.activation(out=warm_out[:], in_=warm[:], func=SILU)
-        w1_raw = [None, None]
         w2_raw = [None, None]
         w3w_raw = tile([P, 2 * N], U8, "w3w_raw")
         nc.sync.dma_start(out=w3w_raw[:].bitcast(I32), in_=w3_words[0].bitcast(I32))
         nc.sync.dma_start(offs_sb[:], offs)
         xw_table = load_words(x_words, "xw_table")
         load_scale_rows(nc.sync, xs_table, x_scales)
-        w1_raw[0] = load_weight_half(w1, 0, "w1_raw0")
+        w1_raw = tile([P, PACK, H], F32, "w1_raw")
+        nc.sync.dma_start(out=w1_raw[:], in_=w1.rearrange("(p j) c -> p j c", j=PACK))
         nc.sync.dma_start(tok_sb[:], tok)
-        w1_raw[1] = load_weight_half(w1, 1, "w1_raw1")
-        w2_raw[0] = load_weight_half(w2, 0, "w2_raw0")
         load_scale_rows(nc.sync, es_table, e_scales)
+        w2_raw[0] = load_weight_half(w2, 0, "w2_raw0")
         w2_raw[1] = load_weight_half(w2, 1, "w2_raw1")
         ew_table = load_words(e_words, "ew_table")
         load_scale_rows(nc.sync, w3s_raw, w3_scales)
         skip_sb = []
-        for piece, cols in enumerate((slice(0, CHUNK), slice(CHUNK, 2 * CHUNK), slice(2 * CHUNK, S))):
+        for piece, cols in enumerate((slice(0, CHUNK), slice(CHUNK, S))):
             part = tile([P, PACK, cols.stop - cols.start], F32, "skip%d" % piece)
             nc.sync.dma_start(out=part[:], in_=skip[:, cols].rearrange("(p t) j -> p t j", t=PACK))
             skip_sb.append(part)
@@ -102,41 +97,37 @@ def tile_picked_zeagle_silu_po_kernel(
         w2_grouped = tile([P, PACK, P, PACK], BF16, "w2_grouped")
         w1_codes = tile([P, H], U32, "w1_codes")
         w2_codes = tile([P, H], U32, "w2_codes")
-        w1_plane = tile([P, H], U8, "w1_plane")
         w2_plane = tile([P, H], U8, "w2_plane")
         w3_codes = tile([P, PACK, P, 2], U8, "w3_codes")
-        w3_plane = tile([P, PACK, P], U8, "w3_plane")
 
         nc.vector.tensor_copy(
             w3_codes[:].rearrange("p t m b -> p m t b"),
             w3w_raw[:].rearrange("p (m t b) -> p m t b", t=PACK, b=2),
         )
-        round_and_deal(nc.scalar.copy, w1_grouped, w1_raw[0], 0, 0, 64)
+        round_and_deal(nc.scalar.copy, w1_grouped, w1_raw, 0, 0, 80)
         nc.vector.tensor_copy(xw_picked[:], xw_table[:].bitcast(U32).indirect(offs_sb[:]))
         nc.vector.tensor_copy(xs_picked[:], xs_table[:].indirect(offs_sb[:]))
-        round_and_deal(nc.vector.tensor_copy, w1_grouped, w1_raw[1], 1, 0, 64)
+        round_and_deal(nc.vector.tensor_copy, w1_grouped, w1_raw, 0, 80, 128)
+        nc.vector.tensor_copy(es_picked[:], es_table[:].indirect(tok_sb[:]))
+        w1_plane = tile([P, H], U8, "w1_plane", tag="es_table")
         nc.vector.quantize_mx(
             out=w1_codes[:].bitcast(FP8X4), scales=w1_plane[:],
             in_=w1_grouped[:].rearrange("p t m j -> p (t m j)"),
         )
-        warm_bank = psum.tile([P, S], F32, name="warm_bank")
-        for t in range(3):
+        warm_bank = psum.tile([P, S], F32, name="post3")
+        for t in range(1):
             wc = slice(t * P, (t + 1) * P)
             nc.tensor.matmul_mx(
                 out=warm_bank[:], lhsT=w1_codes[:, wc].bitcast(FP8X4), lhsT_scale=w1_plane[:, wc],
                 rhs=xw_picked[:].bitcast(FP8X4), rhs_scale=xs_picked[:], start=True, stop=True,
             )
-        nc.vector.tensor_copy(es_picked[:], es_table[:].indirect(tok_sb[:]))
         round_and_deal(nc.scalar.copy, w2_grouped, w2_raw[0], 0, 0, 64)
-        round_and_deal(nc.scalar.copy, w2_grouped, w2_raw[1], 1, 0, 40)
-        round_and_deal(nc.vector.tensor_copy, w2_grouped, w2_raw[1], 1, 40, 64)
-
-        def quantise_w2(pair):
-            cols = slice(pair * 2 * P, (pair + 1) * 2 * P)
-            nc.vector.quantize_mx(
-                out=w2_codes[:, cols].bitcast(FP8X4), scales=w2_plane[:, cols],
-                in_=w2_grouped[:, 2 * pair : 2 * pair + 2, :, :].rearrange("p t m j -> p (t m j)"),
-            )
+        round_and_deal(nc.scalar.copy, w2_grouped, w2_raw[1], 1, 0, 28)
+        round_and_deal(nc.vector.tensor_copy, w2_grouped, w2_raw[1], 1, 28, 64)
+        nc.vector.quantize_mx(
+            out=w2_codes[:].bitcast(FP8X4), scales=w2_plane[:],
+            in_=w2_grouped[:].rearrange("p t m j -> p (t m j)"),
+        )
 
         ew_first = tile([P, CHUNK], U32, "ew_first")
         ew_picked = [ew_first[:]]
@@ -154,7 +145,7 @@ def tile_picked_zeagle_silu_po_kernel(
 
         def first_layer(c):
             cols = slice(c * CHUNK, (c + 1) * CHUNK)
-            bank = psum.tile([P, PACK, CHUNK], F32, name="pre%d" % (c % 2))
+            bank = psum.tile([P, PACK, CHUNK], F32, name="pre%d" % c)
             for t in range(PACK):
                 wc = slice(t * P, (t + 1) * P)
                 nc.tensor.matmul_mx(
@@ -171,7 +162,7 @@ def tile_picked_zeagle_silu_po_kernel(
 
         def second_layer(c):
             cols = slice(c * CHUNK, (c + 1) * CHUNK)
-            h_codes = tile([P, CHUNK], U32, "h_codes%d" % c, tag="skip%d" % (c - 2) if c >= 2 else None)
+            h_codes = tile([P, CHUNK], U32, "h_codes%d" % c, tag="skip0" if c == CHUNKS - 1 else None)
             nc.vector.quantize_mx(
                 out=h_codes[:].bitcast(FP8X4), scales=h_plane[:, cols],
                 in_=h_bf[c][:].rearrange("p n t -> p (n t)"),
@@ -189,7 +180,7 @@ def tile_picked_zeagle_silu_po_kernel(
 
         def add_and_store(c, bank):
             cols = slice(c * CHUNK, (c + 1) * CHUNK)
-            added = skip_sb[c][:] if c < 2 else skip_sb[2][:, :, (c - 2) * CHUNK : (c - 1) * CHUNK]
+            added = skip_sb[0][:] if c == 0 else skip_sb[1][:, :, (c - 1) * CHUNK : c * CHUNK]
             nc.vector.tensor_tensor(y_f32[c][:], bank[:], added, ADD)
             nc.sync.dma_start(out=out_0[:, cols].rearrange("(p t) j -> p t j", t=PACK), in_=y_f32[c][:])
             copy = nc.vector.tensor_copy if c == CHUNKS - 1 else nc.scalar.copy
@@ -205,17 +196,18 @@ def tile_picked_zeagle_silu_po_kernel(
                 in_=y_bf[c][:].rearrange("p n t -> p (n t)"),
             )
             words = out_1[0].rearrange("p c r -> p (c r)").bitcast(I32)
-            nc.sync.dma_start(out=words[:, cols], in_=y_codes[:, cols].bitcast(I32))
+            if c >= CHUNKS - 2:
+                stored = slice(0, S - CHUNK) if c == CHUNKS - 2 else cols
+                nc.sync.dma_start(out=words[:, stored], in_=y_codes[:, stored].bitcast(I32))
 
-        quantise_w2(0)
         gather_e(0)
-        quantise_w2(1)
-        ew_rest = tile([P, S - CHUNK], U32, "ew_rest", tag="w2_grouped")
-        ew_picked.extend(ew_rest[:, c * CHUNK : (c + 1) * CHUNK] for c in range(CHUNKS - 1))
+        ew_middle = tile([P, 3 * CHUNK], U32, "ew_middle", tag="w2_grouped")
+        ew_picked.extend(ew_middle[:, c * CHUNK : (c + 1) * CHUNK] for c in range(3))
         first_layer(0)
         gather_e(1)
         first_layer(1)
         gather_e(2)
+        w3_plane = tile([P, PACK, P], U8, "w3_plane", tag="ew_first")
         nc.vector.tensor_copy(
             w3_plane[:].rearrange("p t m -> p m t"),
             w3s_raw[:].rearrange("p (m t) -> p m t", t=PACK),

@@ -63,7 +63,6 @@ def tile_picked_zeagle_silu_po_kernel(
         nc.gpsimd.memset(xs_table[:].bitcast(I32), 0)
         nc.gpsimd.memset(es_table[:].bitcast(I32), 0)
         nc.gpsimd.memset(w3s_raw[:].bitcast(I32), 0)
-        w2_raw = [None, None]
         w3w_raw = tile([P, 2 * N], U8, "w3w_raw")
         nc.sync.dma_start(out=w3w_raw[:].bitcast(I32), in_=w3_words[0].bitcast(I32))
         nc.sync.dma_start(offs_sb[:], offs)
@@ -73,8 +72,8 @@ def tile_picked_zeagle_silu_po_kernel(
         nc.sync.dma_start(out=w1_raw[:], in_=w1.rearrange("(p j) c -> p j c", j=PACK))
         nc.sync.dma_start(tok_sb[:], tok)
         load_scale_rows(nc.sync, es_table, e_scales)
-        w2_raw[0] = load_weight_half(w2, 0, "w2_raw0")
-        w2_raw[1] = load_weight_half(w2, 1, "w2_raw1")
+        w2_raw = tile([P, PACK, H], F32, "w2_raw")
+        nc.sync.dma_start(out=w2_raw[:], in_=w2.rearrange("(p j) c -> p j c", j=PACK))
         ew_table = load_words(e_words, "ew_table")
         load_scale_rows(nc.sync, w3s_raw, w3_scales)
         skip_sb = []
@@ -104,10 +103,10 @@ def tile_picked_zeagle_silu_po_kernel(
             w3_codes[:].rearrange("p t m b -> p m t b"),
             w3w_raw[:].rearrange("p (m t b) -> p m t b", t=PACK, b=2),
         )
-        round_and_deal(nc.scalar.copy, w1_grouped, w1_raw, 0, 0, 80)
+        round_and_deal(nc.scalar.copy, w1_grouped, w1_raw, 0, 0, 72)
         nc.vector.tensor_copy(xw_picked[:], xw_table[:].bitcast(U32).indirect(offs_sb[:]))
         nc.vector.tensor_copy(xs_picked[:], xs_table[:].indirect(offs_sb[:]))
-        round_and_deal(nc.vector.tensor_copy, w1_grouped, w1_raw, 0, 80, 128)
+        round_and_deal(nc.vector.tensor_copy, w1_grouped, w1_raw, 0, 72, 128)
         nc.vector.tensor_copy(es_picked[:], es_table[:].indirect(tok_sb[:]))
         w1_plane = tile([P, H], U8, "w1_plane", tag="es_table")
         nc.vector.quantize_mx(
@@ -121,15 +120,14 @@ def tile_picked_zeagle_silu_po_kernel(
                 out=warm_bank[:], lhsT=w1_codes[:, wc].bitcast(FP8X4), lhsT_scale=w1_plane[:, wc],
                 rhs=xw_picked[:].bitcast(FP8X4), rhs_scale=xs_picked[:], start=True, stop=True,
             )
-        round_and_deal(nc.scalar.copy, w2_grouped, w2_raw[0], 0, 0, 64)
-        round_and_deal(nc.scalar.copy, w2_grouped, w2_raw[1], 1, 0, 28)
-        round_and_deal(nc.vector.tensor_copy, w2_grouped, w2_raw[1], 1, 28, 64)
+        round_and_deal(nc.scalar.copy, w2_grouped, w2_raw, 0, 0, 56)
+        round_and_deal(nc.vector.tensor_copy, w2_grouped, w2_raw, 0, 56, 128)
         nc.vector.quantize_mx(
             out=w2_codes[:].bitcast(FP8X4), scales=w2_plane[:],
             in_=w2_grouped[:].rearrange("p t m j -> p (t m j)"),
         )
 
-        ew_first = tile([P, CHUNK], U32, "ew_first")
+        ew_first = tile([P, CHUNK], U32, "ew_first", tag="w2_raw")
         ew_picked = [ew_first[:]]
 
         def gather_e(c):
@@ -207,7 +205,7 @@ def tile_picked_zeagle_silu_po_kernel(
         gather_e(1)
         first_layer(1)
         gather_e(2)
-        w3_plane = tile([P, PACK, P], U8, "w3_plane", tag="ew_first")
+        w3_plane = tile([P, PACK, P], U8, "w3_plane", tag="w2_raw")
         nc.vector.tensor_copy(
             w3_plane[:].rearrange("p t m -> p m t"),
             w3s_raw[:].rearrange("p (m t) -> p m t", t=PACK),

@@ -61,110 +61,112 @@ def tile_picked_zeagle_silu_po_kernel(
         w3s_raw = tile([P, N], U8, "w3s_raw")
 
         nc.gpsimd.memset(xs_table[:].bitcast(I32), 0)
+        warm = tile([P, 2], F32, "warm")
+        nc.gpsimd.memset(warm[:, 0:1], 0.0)
         nc.gpsimd.memset(es_table[:].bitcast(I32), 0)
         nc.gpsimd.memset(w3s_raw[:].bitcast(I32), 0)
-        w3w_raw = tile([P, 2 * N], U8, "w3w_raw")
-        nc.sync.dma_start(out=w3w_raw[:].bitcast(I32), in_=w3_words[0].bitcast(I32))
         nc.sync.dma_start(offs_sb[:], offs)
+        nc.sync.dma_start(tok_sb[:], tok)
         xw_table = load_words(x_words, "xw_table")
         load_scale_rows(nc.sync, xs_table, x_scales)
-        w1_raw = tile([P, PACK, H], F32, "w1_raw")
-        nc.sync.dma_start(out=w1_raw[:], in_=w1.rearrange("(p j) c -> p j c", j=PACK))
-        nc.sync.dma_start(tok_sb[:], tok)
+        w1_raw = [load_weight_half(w1, half, "w1_raw%d" % half) for half in range(2)]
         load_scale_rows(nc.sync, es_table, e_scales)
-        w2_raw = tile([P, PACK, H], F32, "w2_raw")
-        nc.sync.dma_start(out=w2_raw[:], in_=w2.rearrange("(p j) c -> p j c", j=PACK))
+        w2_raw = [load_weight_half(w2, half, "w2_raw%d" % half) for half in range(2)]
         ew_table = load_words(e_words, "ew_table")
-        load_scale_rows(nc.sync, w3s_raw, w3_scales)
-        skip_sb = []
-        for piece, cols in enumerate((slice(0, CHUNK), slice(CHUNK, S))):
+        w3w_raw = tile([P, 2 * N], U8, "w3w_raw")
+        nc.sync.dma_start(out=w3w_raw[:].bitcast(I32), in_=w3_words[0].bitcast(I32))
+        skip_sb = {}
+        for piece, cols in ((0, slice(0, CHUNK)), (1, slice(CHUNK, S))):
             part = tile([P, PACK, cols.stop - cols.start], F32, "skip%d" % piece)
             nc.sync.dma_start(out=part[:], in_=skip[:, cols].rearrange("(p t) j -> p t j", t=PACK))
-            skip_sb.append(part)
+            skip_sb[piece] = part
+            if piece == 0:
+                load_scale_rows(nc.sync, w3s_raw, w3_scales)
 
         def round_and_deal(copy, grouped, raw, half, first, last):
             m0 = half * HALF // PACK
             copy(
                 out=grouped[:, :, m0 + first : m0 + last, :].rearrange("p t m j -> p m j t"),
-                in_=raw[:].rearrange("p j (m t) -> p m j t", t=PACK)[:, first:last, :, :],
+                in_=raw[half][:].rearrange("p j (m t) -> p m j t", t=PACK)[:, first:last, :, :],
             )
 
+        def quantise(codes, plane, values):
+            nc.vector.quantize_mx(out=codes.bitcast(FP8X4), scales=plane, in_=values)
+
         xs_picked = tile([P, S], U8, "xs_picked")
-        es_picked = tile([P, S], U8, "es_picked")
-        xw_picked = tile([P, S], U32, "xw_picked")
         w1_grouped = tile([P, PACK, P, PACK], BF16, "w1_grouped")
         w2_grouped = tile([P, PACK, P, PACK], BF16, "w2_grouped")
         w1_codes = tile([P, H], U32, "w1_codes")
         w2_codes = tile([P, H], U32, "w2_codes")
         w2_plane = tile([P, H], U8, "w2_plane")
         w3_codes = tile([P, PACK, P, 2], U8, "w3_codes")
+        nc.scalar.activation(out=warm[:, 1:2], in_=warm[:, 0:1], func=SILU)
 
-        nc.vector.tensor_copy(
-            w3_codes[:].rearrange("p t m b -> p m t b"),
-            w3w_raw[:].rearrange("p (m t b) -> p m t b", t=PACK, b=2),
-        )
-        round_and_deal(nc.scalar.copy, w1_grouped, w1_raw, 0, 0, 72)
+        xw_picked = tile([P, S], U32, "xw_picked")
+        es_picked = tile([P, S], U8, "es_picked")
         nc.vector.tensor_copy(xw_picked[:], xw_table[:].bitcast(U32).indirect(offs_sb[:]))
         nc.vector.tensor_copy(xs_picked[:], xs_table[:].indirect(offs_sb[:]))
-        round_and_deal(nc.vector.tensor_copy, w1_grouped, w1_raw, 0, 72, 128)
+        round_and_deal(nc.scalar.copy, w1_grouped, w1_raw, 0, 0, 64)
+        round_and_deal(nc.scalar.copy, w1_grouped, w1_raw, 1, 0, 64)
         nc.vector.tensor_copy(es_picked[:], es_table[:].indirect(tok_sb[:]))
         w1_plane = tile([P, H], U8, "w1_plane", tag="es_table")
-        nc.vector.quantize_mx(
-            out=w1_codes[:].bitcast(FP8X4), scales=w1_plane[:],
-            in_=w1_grouped[:].rearrange("p t m j -> p (t m j)"),
-        )
+        quantise(w1_codes[:], w1_plane[:], w1_grouped[:].rearrange("p t m j -> p (t m j)"))
         warm_bank = psum.tile([P, S], F32, name="post3")
-        for t in range(1):
+        for t in range(2):
             wc = slice(t * P, (t + 1) * P)
             nc.tensor.matmul_mx(
                 out=warm_bank[:], lhsT=w1_codes[:, wc].bitcast(FP8X4), lhsT_scale=w1_plane[:, wc],
-                rhs=xw_picked[:].bitcast(FP8X4), rhs_scale=xs_picked[:], start=True, stop=True,
+                rhs=w1_codes[:].bitcast(FP8X4), rhs_scale=w1_plane[:], start=True, stop=True,
             )
-        round_and_deal(nc.scalar.copy, w2_grouped, w2_raw, 0, 0, 56)
-        round_and_deal(nc.vector.tensor_copy, w2_grouped, w2_raw, 0, 56, 128)
-        nc.vector.quantize_mx(
-            out=w2_codes[:].bitcast(FP8X4), scales=w2_plane[:],
-            in_=w2_grouped[:].rearrange("p t m j -> p (t m j)"),
-        )
+        round_and_deal(nc.scalar.copy, w2_grouped, w2_raw, 0, 0, 64)
+        round_and_deal(nc.scalar.copy, w2_grouped, w2_raw, 1, 0, 16)
+        round_and_deal(nc.vector.tensor_copy, w2_grouped, w2_raw, 1, 16, 64)
+        quantise(w2_codes[:], w2_plane[:], w2_grouped[:].rearrange("p t m j -> p (t m j)"))
 
-        ew_first = tile([P, CHUNK], U32, "ew_first", tag="w2_raw")
-        ew_picked = [ew_first[:]]
+        ew_first = tile([P, CHUNK], U32, "ew_first", tag="w2_raw1")
+        ew_rest = tile([P, S - CHUNK], U32, "ew_rest", tag="w2_grouped")
+        ew_picked = [ew_first[:]] + [ew_rest[:, c * CHUNK : (c + 1) * CHUNK] for c in range(CHUNKS - 1)]
 
         def gather_e(c):
             entries = tok_sb[:, c * LIST_COLS : (c + 1) * LIST_COLS]
             nc.vector.tensor_copy(ew_picked[c], ew_table[:].bitcast(U32).indirect(entries))
 
-        h_plane = tile([P, S], U8, "h_plane")
         y_codes = tile([P, S], U32, "y_codes")
         y_plane = tile([P, S], U8, "y_plane")
         h_bf = [tile([P, CHUNK, PACK], BF16, "h_bf%d" % c) for c in range(CHUNKS)]
         y_bf = [tile([P, CHUNK, PACK], BF16, "y_bf%d" % c) for c in range(CHUNKS)]
         y_f32 = [tile([P, PACK, CHUNK], F32, "y_f32%d" % c) for c in range(CHUNKS)]
+        pre = [psum.tile([P, PACK, CHUNK], F32, name="pre%d" % c) for c in range(CHUNKS)]
+
+        def x_pass(c, t):
+            cols = slice(c * CHUNK, (c + 1) * CHUNK)
+            wc = slice(t * P, (t + 1) * P)
+            nc.tensor.matmul_mx(
+                out=pre[c][:, t, :], lhsT=w1_codes[:, wc].bitcast(FP8X4), lhsT_scale=w1_plane[:, wc],
+                rhs=xw_picked[:, cols].bitcast(FP8X4), rhs_scale=xs_picked[:, cols],
+                start=True, stop=False,
+            )
+
+        def e_pass(c, t):
+            cols = slice(c * CHUNK, (c + 1) * CHUNK)
+            wc = slice(t * P, (t + 1) * P)
+            nc.tensor.matmul_mx(
+                out=pre[c][:, t, :], lhsT=w2_codes[:, wc].bitcast(FP8X4), lhsT_scale=w2_plane[:, wc],
+                rhs=ew_picked[c].bitcast(FP8X4), rhs_scale=es_picked[:, cols],
+                start=False, stop=True,
+            )
 
         def first_layer(c):
-            cols = slice(c * CHUNK, (c + 1) * CHUNK)
-            bank = psum.tile([P, PACK, CHUNK], F32, name="pre%d" % c)
             for t in range(PACK):
-                wc = slice(t * P, (t + 1) * P)
-                nc.tensor.matmul_mx(
-                    out=bank[:, t, :], lhsT=w1_codes[:, wc].bitcast(FP8X4), lhsT_scale=w1_plane[:, wc],
-                    rhs=xw_picked[:, cols].bitcast(FP8X4), rhs_scale=xs_picked[:, cols],
-                    start=True, stop=False,
-                )
-                nc.tensor.matmul_mx(
-                    out=bank[:, t, :], lhsT=w2_codes[:, wc].bitcast(FP8X4), lhsT_scale=w2_plane[:, wc],
-                    rhs=ew_picked[c].bitcast(FP8X4), rhs_scale=es_picked[:, cols],
-                    start=False, stop=True,
-                )
-            nc.scalar.activation(out=h_bf[c][:], in_=bank[:].rearrange("p t n -> p n t"), func=SILU)
+                if t > 0:
+                    x_pass(c, t)
+                e_pass(c, t)
+            nc.scalar.activation(out=h_bf[c][:], in_=pre[c][:].rearrange("p t n -> p n t"), func=SILU)
 
         def second_layer(c):
             cols = slice(c * CHUNK, (c + 1) * CHUNK)
             h_codes = tile([P, CHUNK], U32, "h_codes%d" % c, tag="skip0" if c == CHUNKS - 1 else None)
-            nc.vector.quantize_mx(
-                out=h_codes[:].bitcast(FP8X4), scales=h_plane[:, cols],
-                in_=h_bf[c][:].rearrange("p n t -> p (n t)"),
-            )
+            quantise(h_codes[:], h_plane[:, cols], h_bf[c][:].rearrange("p n t -> p (n t)"))
             bank = psum.tile([P, PACK, CHUNK], F32, name="post%d" % c)
             for t in range(PACK):
                 nc.tensor.matmul_mx(
@@ -189,28 +191,28 @@ def tile_picked_zeagle_silu_po_kernel(
 
         def quantise_out(c):
             cols = slice(c * CHUNK, (c + 1) * CHUNK)
-            nc.vector.quantize_mx(
-                out=y_codes[:, cols].bitcast(FP8X4), scales=y_plane[:, cols],
-                in_=y_bf[c][:].rearrange("p n t -> p (n t)"),
-            )
+            quantise(y_codes[:, cols], y_plane[:, cols], y_bf[c][:].rearrange("p n t -> p (n t)"))
             words = out_1[0].rearrange("p c r -> p (c r)").bitcast(I32)
             if c >= CHUNKS - 2:
                 stored = slice(0, S - CHUNK) if c == CHUNKS - 2 else cols
                 nc.sync.dma_start(out=words[:, stored], in_=y_codes[:, stored].bitcast(I32))
 
-        gather_e(0)
-        ew_middle = tile([P, 3 * CHUNK], U32, "ew_middle", tag="w2_grouped")
-        ew_picked.extend(ew_middle[:, c * CHUNK : (c + 1) * CHUNK] for c in range(3))
+        for c in range(CHUNKS):
+            x_pass(c, 0)
+        for c in range(CHUNKS):
+            gather_e(c)
+        nc.vector.tensor_copy(
+            w3_codes[:].rearrange("p t m b -> p m t b"),
+            w3w_raw[:].rearrange("p (m t b) -> p m t b", t=PACK, b=2),
+        )
         first_layer(0)
-        gather_e(1)
-        first_layer(1)
-        gather_e(2)
-        w3_plane = tile([P, PACK, P], U8, "w3_plane", tag="w2_raw")
+        w3_plane = tile([P, PACK, P], U8, "w3_plane", tag="w2_raw1")
         nc.vector.tensor_copy(
             w3_plane[:].rearrange("p t m -> p m t"),
             w3s_raw[:].rearrange("p (m t) -> p m t", t=PACK),
         )
-        gather_e(3)
+        h_plane = tile([P, S], U8, "h_plane", tag="w3s_raw")
+        first_layer(1)
         banks = {}
         for step in range(CHUNKS + 2):
             if step < CHUNKS:

@@ -37,10 +37,10 @@ def tile_picked_zeagle_silu_po_kernel(
             return keep.tile(shape, dtype, name=name, tag=tag or name, align_bytes=64)
 
         def load_scale_rows(queue, plane, rows):
-            for q in range(4):
+            for r in range(4):
                 queue.dma_start(
-                    out=plane[32 * q : 32 * q + 4, :].bitcast(I32),
-                    in_=rows[0, 4 * q : 4 * q + 4, :].bitcast(I32),
+                    out=plane[r:P:32, :].bitcast(I32),
+                    in_=rows[0, r:16:4, :].bitcast(I32),
                 )
 
         def load_weight_half(w, half, name):
@@ -66,8 +66,8 @@ def tile_picked_zeagle_silu_po_kernel(
         nc.gpsimd.memset(es_table[:].bitcast(I32), 0)
         nc.gpsimd.memset(w3s_raw[:].bitcast(I32), 0)
         nc.sync.dma_start(offs_sb[:], offs)
-        nc.sync.dma_start(tok_sb[:], tok)
         xw_table = load_words(x_words, "xw_table")
+        nc.sync.dma_start(tok_sb[:], tok)
         load_scale_rows(nc.sync, xs_table, x_scales)
         w1_raw = [load_weight_half(w1, half, "w1_raw%d" % half) for half in range(2)]
         load_scale_rows(nc.sync, es_table, e_scales)
@@ -107,25 +107,25 @@ def tile_picked_zeagle_silu_po_kernel(
         nc.vector.tensor_copy(xw_picked[:], xw_table[:].bitcast(U32).indirect(offs_sb[:]))
         nc.vector.tensor_copy(xs_picked[:], xs_table[:].indirect(offs_sb[:]))
         round_and_deal(nc.scalar.copy, w1_grouped, w1_raw, 0, 0, 64)
-        round_and_deal(nc.scalar.copy, w1_grouped, w1_raw, 1, 0, 64)
+        round_and_deal(nc.scalar.copy, w1_grouped, w1_raw, 1, 0, 44)
+        round_and_deal(nc.vector.tensor_copy, w1_grouped, w1_raw, 1, 44, 64)
         nc.vector.tensor_copy(es_picked[:], es_table[:].indirect(tok_sb[:]))
         w1_plane = tile([P, H], U8, "w1_plane", tag="es_table")
         quantise(w1_codes[:], w1_plane[:], w1_grouped[:].rearrange("p t m j -> p (t m j)"))
         warm_bank = psum.tile([P, S], F32, name="post3")
-        for t in range(2):
+        for t in range(3):
             wc = slice(t * P, (t + 1) * P)
             nc.tensor.matmul_mx(
-                out=warm_bank[:], lhsT=w1_codes[:, wc].bitcast(FP8X4), lhsT_scale=w1_plane[:, wc],
-                rhs=w1_codes[:].bitcast(FP8X4), rhs_scale=w1_plane[:], start=True, stop=True,
+                out=warm_bank[:], lhsT=xw_picked[:, wc].bitcast(FP8X4), lhsT_scale=xs_picked[:, wc],
+                rhs=xw_picked[:].bitcast(FP8X4), rhs_scale=es_picked[:], start=True, stop=True,
             )
         round_and_deal(nc.scalar.copy, w2_grouped, w2_raw, 0, 0, 64)
         round_and_deal(nc.scalar.copy, w2_grouped, w2_raw, 1, 0, 16)
         round_and_deal(nc.vector.tensor_copy, w2_grouped, w2_raw, 1, 16, 64)
         quantise(w2_codes[:], w2_plane[:], w2_grouped[:].rearrange("p t m j -> p (t m j)"))
 
-        ew_first = tile([P, CHUNK], U32, "ew_first", tag="w2_raw1")
-        ew_rest = tile([P, S - CHUNK], U32, "ew_rest", tag="w2_grouped")
-        ew_picked = [ew_first[:]] + [ew_rest[:, c * CHUNK : (c + 1) * CHUNK] for c in range(CHUNKS - 1)]
+        ew_all = tile([P, S], U32, "ew_all", tag="w2_raw1")
+        ew_picked = [ew_all[:, c * CHUNK : (c + 1) * CHUNK] for c in range(CHUNKS)]
 
         def gather_e(c):
             entries = tok_sb[:, c * LIST_COLS : (c + 1) * LIST_COLS]
@@ -134,7 +134,8 @@ def tile_picked_zeagle_silu_po_kernel(
         y_codes = tile([P, S], U32, "y_codes")
         y_plane = tile([P, S], U8, "y_plane")
         h_bf = [tile([P, CHUNK, PACK], BF16, "h_bf%d" % c) for c in range(CHUNKS)]
-        y_bf = [tile([P, CHUNK, PACK], BF16, "y_bf%d" % c) for c in range(CHUNKS)]
+        y_bf_all = tile([P, S, PACK], BF16, "y_bf")
+        y_bf = [y_bf_all[:, c * CHUNK : (c + 1) * CHUNK, :] for c in range(CHUNKS)]
         y_f32 = [tile([P, PACK, CHUNK], F32, "y_f32%d" % c) for c in range(CHUNKS)]
         pre = [psum.tile([P, PACK, CHUNK], F32, name="pre%d" % c) for c in range(CHUNKS)]
 
@@ -165,7 +166,7 @@ def tile_picked_zeagle_silu_po_kernel(
 
         def second_layer(c):
             cols = slice(c * CHUNK, (c + 1) * CHUNK)
-            h_codes = tile([P, CHUNK], U32, "h_codes%d" % c, tag="skip0" if c == CHUNKS - 1 else None)
+            h_codes = tile([P, CHUNK], U32, "h_codes%d" % c, tag="h_codes%d" % (c % 2))
             quantise(h_codes[:], h_plane[:, cols], h_bf[c][:].rearrange("p n t -> p (n t)"))
             bank = psum.tile([P, PACK, CHUNK], F32, name="post%d" % c)
             for t in range(PACK):
@@ -185,17 +186,13 @@ def tile_picked_zeagle_silu_po_kernel(
             nc.sync.dma_start(out=out_0[:, cols].rearrange("(p t) j -> p t j", t=PACK), in_=y_f32[c][:])
             copy = nc.vector.tensor_copy if c == CHUNKS - 1 else nc.scalar.copy
             copy(
-                out=y_bf[c][:].rearrange("p (g i) t -> p g t i", i=4),
+                out=y_bf[c].rearrange("p (g i) t -> p g t i", i=4),
                 in_=y_f32[c][:].rearrange("p t (g i) -> p g t i", i=4),
             )
 
-        def quantise_out(c):
-            cols = slice(c * CHUNK, (c + 1) * CHUNK)
-            quantise(y_codes[:, cols], y_plane[:, cols], y_bf[c][:].rearrange("p n t -> p (n t)"))
-            words = out_1[0].rearrange("p c r -> p (c r)").bitcast(I32)
-            if c >= CHUNKS - 2:
-                stored = slice(0, S - CHUNK) if c == CHUNKS - 2 else cols
-                nc.sync.dma_start(out=words[:, stored], in_=y_codes[:, stored].bitcast(I32))
+        def quantise_out(first, last):
+            cols = slice(first * CHUNK, last * CHUNK)
+            quantise(y_codes[:, cols], y_plane[:, cols], y_bf_all[:, cols, :].rearrange("p n t -> p (n t)"))
 
         for c in range(CHUNKS):
             x_pass(c, 0)
@@ -206,26 +203,28 @@ def tile_picked_zeagle_silu_po_kernel(
             w3w_raw[:].rearrange("p (m t b) -> p m t b", t=PACK, b=2),
         )
         first_layer(0)
-        w3_plane = tile([P, PACK, P], U8, "w3_plane", tag="w2_raw1")
+        w3_plane = tile([P, PACK, P], U8, "w3_plane")
         nc.vector.tensor_copy(
             w3_plane[:].rearrange("p t m -> p m t"),
             w3s_raw[:].rearrange("p (m t) -> p m t", t=PACK),
         )
         h_plane = tile([P, S], U8, "h_plane", tag="w3s_raw")
         first_layer(1)
-        banks = {}
-        for step in range(CHUNKS + 2):
-            if step < CHUNKS:
-                banks[step] = second_layer(step)
-            if step + 2 < CHUNKS:
-                first_layer(step + 2)
-            if 0 <= step - 2 < CHUNKS:
-                quantise_out(step - 2)
-            if 0 <= step - 1 < CHUNKS:
-                add_and_store(step - 1, banks[step - 1])
+        first_layer(2)
+        first_layer(3)
+        banks = [second_layer(c) for c in range(CHUNKS - 1)]
+        add_and_store(0, banks[0])
+        banks.append(second_layer(CHUNKS - 1))
+        for c in range(1, CHUNKS):
+            add_and_store(c, banks[c])
+        quantise_out(0, 2)
+        quantise_out(2, 3)
+        quantise_out(3, 4)
+        words = out_1[0].rearrange("p c r -> p (c r)").bitcast(I32)
+        nc.sync.dma_start(out=words, in_=y_codes[:].bitcast(I32))
         for q in range(4):
             queue = nc.scalar if q % 2 else nc.sync
             queue.dma_start(
-                out=out_2[0, 4 * q : 4 * q + 4, :].bitcast(I32),
-                in_=y_plane[32 * q : 32 * q + 4, :].bitcast(I32),
+                out=out_2[0, q:16:4, :].bitcast(I32),
+                in_=y_plane[q:P:32, :].bitcast(I32),
             )

@@ -65,16 +65,16 @@ def tile_picked_zeagle_silu_po_kernel(
         nc.gpsimd.memset(warm[:, 0:1], 0.0)
         nc.gpsimd.memset(es_table[:].bitcast(I32), 0)
         nc.gpsimd.memset(w3s_raw[:].bitcast(I32), 0)
+        w3w_raw = tile([P, 2 * N], U8, "w3w_raw")
+        nc.sync.dma_start(out=w3w_raw[:].bitcast(I32), in_=w3_words[0].bitcast(I32))
         nc.sync.dma_start(offs_sb[:], offs)
         xw_table = load_words(x_words, "xw_table")
-        nc.sync.dma_start(tok_sb[:], tok)
         load_scale_rows(nc.sync, xs_table, x_scales)
         w1_raw = [load_weight_half(w1, half, "w1_raw%d" % half) for half in range(2)]
+        nc.sync.dma_start(tok_sb[:], tok)
         load_scale_rows(nc.sync, es_table, e_scales)
         w2_raw = [load_weight_half(w2, half, "w2_raw%d" % half) for half in range(2)]
         ew_table = load_words(e_words, "ew_table")
-        w3w_raw = tile([P, 2 * N], U8, "w3w_raw")
-        nc.sync.dma_start(out=w3w_raw[:].bitcast(I32), in_=w3_words[0].bitcast(I32))
         skip_sb = {}
         for piece, cols in ((0, slice(0, CHUNK)), (1, slice(CHUNK, S))):
             part = tile([P, PACK, cols.stop - cols.start], F32, "skip%d" % piece)
@@ -102,6 +102,10 @@ def tile_picked_zeagle_silu_po_kernel(
         w3_codes = tile([P, PACK, P, 2], U8, "w3_codes")
         nc.scalar.activation(out=warm[:, 1:2], in_=warm[:, 0:1], func=SILU)
 
+        nc.vector.tensor_copy(
+            w3_codes[:],
+            w3w_raw[:].rearrange("p (m t b) -> p t m b", t=PACK, b=2),
+        )
         xw_picked = tile([P, S], U32, "xw_picked")
         es_picked = tile([P, S], U8, "es_picked")
         nc.vector.tensor_copy(xw_picked[:], xw_table[:].bitcast(U32).indirect(offs_sb[:]))
@@ -127,9 +131,10 @@ def tile_picked_zeagle_silu_po_kernel(
         ew_all = tile([P, S], U32, "ew_all", tag="w2_raw1")
         ew_picked = [ew_all[:, c * CHUNK : (c + 1) * CHUNK] for c in range(CHUNKS)]
 
-        def gather_e(c):
-            entries = tok_sb[:, c * LIST_COLS : (c + 1) * LIST_COLS]
-            nc.vector.tensor_copy(ew_picked[c], ew_table[:].bitcast(U32).indirect(entries))
+        def gather_e(first, last):
+            entries = tok_sb[:, first * LIST_COLS : last * LIST_COLS]
+            picked = ew_all[:, first * CHUNK : last * CHUNK]
+            nc.vector.tensor_copy(picked, ew_table[:].bitcast(U32).indirect(entries))
 
         y_codes = tile([P, S], U32, "y_codes")
         y_plane = tile([P, S], U8, "y_plane")
@@ -196,17 +201,14 @@ def tile_picked_zeagle_silu_po_kernel(
 
         for c in range(CHUNKS):
             x_pass(c, 0)
-        for c in range(CHUNKS):
-            gather_e(c)
-        nc.vector.tensor_copy(
-            w3_codes[:].rearrange("p t m b -> p m t b"),
-            w3w_raw[:].rearrange("p (m t b) -> p m t b", t=PACK, b=2),
-        )
+        gather_e(0, 1)
+        gather_e(1, 2)
+        gather_e(2, 4)
         first_layer(0)
         w3_plane = tile([P, PACK, P], U8, "w3_plane")
         nc.vector.tensor_copy(
-            w3_plane[:].rearrange("p t m -> p m t"),
-            w3s_raw[:].rearrange("p (m t) -> p m t", t=PACK),
+            w3_plane[:],
+            w3s_raw[:].rearrange("p (m t) -> p t m", t=PACK),
         )
         h_plane = tile([P, S], U8, "h_plane", tag="w3s_raw")
         first_layer(1)

@@ -18,10 +18,17 @@ ADD = mybir.AluOpType.add
 
 P = 128
 PACK = 4
+QUADRANT = 32
+SCALE_ROWS = 16
 CHUNK = 128
 CHUNKS = S // CHUNK
+LAST = CHUNKS - 1
 LIST_COLS = CHUNK // 16
 HALF = H // 2
+GROUPS = HALF // PACK
+W1_SCALAR_GROUPS = 28
+W2_SCALAR_GROUPS = 22
+WARM_UP_PASSES = 3
 
 
 def tile_picked_zeagle_silu_po_kernel(
@@ -36,18 +43,26 @@ def tile_picked_zeagle_silu_po_kernel(
         def tile(shape, dtype, name, tag=None):
             return keep.tile(shape, dtype, name=name, tag=tag or name, align_bytes=64)
 
-        def load_scale_rows(queue, plane, rows):
-            for r in range(4):
-                queue.dma_start(
-                    out=plane[r:P:32, :].bitcast(I32),
-                    in_=rows[0, r:16:4, :].bitcast(I32),
+        def columns(first, last):
+            return slice(first * CHUNK, last * CHUNK)
+
+        def entries(list_tile, first, last):
+            return list_tile[:, first * LIST_COLS : last * LIST_COLS]
+
+        def load_scale_rows(plane, rows):
+            for r in range(PACK):
+                nc.sync.dma_start(
+                    out=plane[r:P:QUADRANT, :].bitcast(I32),
+                    in_=rows[0, r:SCALE_ROWS:PACK, :].bitcast(I32),
                 )
 
-        def load_weight_half(w, half, name):
-            raw = tile([P, PACK, HALF], F32, name)
-            cols = slice(half * HALF, (half + 1) * HALF)
-            nc.sync.dma_start(out=raw[:], in_=w[:, cols].rearrange("(p j) c -> p j c", j=PACK))
+        def load_rows(matrix, cols, name):
+            raw = tile([P, PACK, cols.stop - cols.start], F32, name)
+            nc.sync.dma_start(out=raw[:], in_=matrix[:, cols].rearrange("(p j) c -> p j c", j=PACK))
             return raw
+
+        def load_halves(w, name):
+            return [load_rows(w, slice(half * HALF, (half + 1) * HALF), name + str(half)) for half in range(2)]
 
         def load_words(words, name):
             table = tile([P, T], I32, name)
@@ -60,35 +75,34 @@ def tile_picked_zeagle_silu_po_kernel(
         es_table = tile([P, T], U8, "es_table")
         w3s_raw = tile([P, N], U8, "w3s_raw")
 
-        nc.gpsimd.memset(xs_table[:].bitcast(I32), 0)
-        warm = tile([P, 2], F32, "warm")
-        nc.gpsimd.memset(warm[:, 0:1], 0.0)
-        nc.gpsimd.memset(es_table[:].bitcast(I32), 0)
-        nc.gpsimd.memset(w3s_raw[:].bitcast(I32), 0)
+        for plane in (xs_table, es_table, w3s_raw):
+            nc.gpsimd.memset(plane[:].bitcast(I32), 0)
+
         w3w_raw = tile([P, 2 * N], U8, "w3w_raw")
         nc.sync.dma_start(out=w3w_raw[:].bitcast(I32), in_=w3_words[0].bitcast(I32))
         nc.sync.dma_start(offs_sb[:], offs)
         xw_table = load_words(x_words, "xw_table")
-        load_scale_rows(nc.sync, xs_table, x_scales)
-        w1_raw = [load_weight_half(w1, half, "w1_raw%d" % half) for half in range(2)]
+        load_scale_rows(xs_table, x_scales)
+        w1_raw = load_halves(w1, "w1_raw")
         nc.sync.dma_start(tok_sb[:], tok)
-        load_scale_rows(nc.sync, es_table, e_scales)
-        w2_raw = [load_weight_half(w2, half, "w2_raw%d" % half) for half in range(2)]
+        load_scale_rows(es_table, e_scales)
+        w2_raw = load_halves(w2, "w2_raw")
         ew_table = load_words(e_words, "ew_table")
-        skip_sb = {}
-        for piece, cols in ((0, slice(0, CHUNK)), (1, slice(CHUNK, S))):
-            part = tile([P, PACK, cols.stop - cols.start], F32, "skip%d" % piece)
-            nc.sync.dma_start(out=part[:], in_=skip[:, cols].rearrange("(p t) j -> p t j", t=PACK))
-            skip_sb[piece] = part
-            if piece == 0:
-                load_scale_rows(nc.sync, w3s_raw, w3_scales)
+        skip_first = load_rows(skip, columns(0, 1), "skip_first")
+        load_scale_rows(w3s_raw, w3_scales)
+        skip_rest = load_rows(skip, columns(1, CHUNKS), "skip_rest")
 
         def round_and_deal(copy, grouped, raw, half, first, last):
-            m0 = half * HALF // PACK
+            g0 = half * GROUPS
             copy(
-                out=grouped[:, :, m0 + first : m0 + last, :].rearrange("p t m j -> p m j t"),
-                in_=raw[half][:].rearrange("p j (m t) -> p m j t", t=PACK)[:, first:last, :, :],
+                out=grouped[:, :, g0 + first : g0 + last, :].rearrange("p t g j -> p g j t"),
+                in_=raw[half][:].rearrange("p j (g t) -> p g j t", t=PACK)[:, first:last, :, :],
             )
+
+        def round_weight(grouped, raw, scalar_groups):
+            round_and_deal(nc.scalar.copy, grouped, raw, 0, 0, GROUPS)
+            round_and_deal(nc.scalar.copy, grouped, raw, 1, 0, scalar_groups)
+            round_and_deal(nc.vector.tensor_copy, grouped, raw, 1, scalar_groups, GROUPS)
 
         def quantise(codes, plane, values):
             nc.vector.quantize_mx(out=codes.bitcast(FP8X4), scales=plane, in_=values)
@@ -100,65 +114,59 @@ def tile_picked_zeagle_silu_po_kernel(
         w2_codes = tile([P, H], U32, "w2_codes")
         w2_plane = tile([P, H], U8, "w2_plane")
         w3_codes = tile([P, PACK, P, 2], U8, "w3_codes")
-        nc.scalar.activation(out=warm[:, 1:2], in_=warm[:, 0:1], func=SILU)
 
-        nc.vector.tensor_copy(
-            w3_codes[:],
-            w3w_raw[:].rearrange("p (m t b) -> p t m b", t=PACK, b=2),
-        )
+        nc.vector.tensor_copy(w3_codes[:], w3w_raw[:].rearrange("p (g t b) -> p t g b", t=PACK, b=2))
         xw_picked = tile([P, S], U32, "xw_picked")
-        es_picked = tile([P, S], U8, "es_picked")
         nc.vector.tensor_copy(xw_picked[:], xw_table[:].bitcast(U32).indirect(offs_sb[:]))
         nc.vector.tensor_copy(xs_picked[:], xs_table[:].indirect(offs_sb[:]))
-        round_and_deal(nc.scalar.copy, w1_grouped, w1_raw, 0, 0, 64)
-        round_and_deal(nc.scalar.copy, w1_grouped, w1_raw, 1, 0, 44)
-        round_and_deal(nc.vector.tensor_copy, w1_grouped, w1_raw, 1, 44, 64)
-        nc.vector.tensor_copy(es_picked[:], es_table[:].indirect(tok_sb[:]))
-        w1_plane = tile([P, H], U8, "w1_plane", tag="es_table")
-        quantise(w1_codes[:], w1_plane[:], w1_grouped[:].rearrange("p t m j -> p (t m j)"))
-        warm_bank = psum.tile([P, S], F32, name="post3")
-        for t in range(3):
-            wc = slice(t * P, (t + 1) * P)
+        round_weight(w1_grouped, w1_raw, W1_SCALAR_GROUPS)
+        w1_plane = tile([P, H], U8, "w1_plane")
+        quantise(w1_codes[:], w1_plane[:], w1_grouped[:].rearrange("p t g j -> p (t g j)"))
+        es_early = tile([P, LAST * CHUNK], U8, "es_early", tag="w1_raw1")
+        nc.vector.tensor_copy(es_early[:], es_table[:].indirect(entries(tok_sb, 0, LAST)))
+
+        warm_bank = psum.tile([P, S], F32, name="post%d" % LAST)
+        for t in range(WARM_UP_PASSES):
+            places = slice(t * P, (t + 1) * P)
             nc.tensor.matmul_mx(
-                out=warm_bank[:], lhsT=xw_picked[:, wc].bitcast(FP8X4), lhsT_scale=xs_picked[:, wc],
-                rhs=xw_picked[:].bitcast(FP8X4), rhs_scale=es_picked[:], start=True, stop=True,
+                out=warm_bank[:], lhsT=w1_codes[:, places].bitcast(FP8X4), lhsT_scale=w1_plane[:, places],
+                rhs=xw_picked[:].bitcast(FP8X4), rhs_scale=xs_picked[:], start=True, stop=True,
             )
-        round_and_deal(nc.scalar.copy, w2_grouped, w2_raw, 0, 0, 64)
-        round_and_deal(nc.scalar.copy, w2_grouped, w2_raw, 1, 0, 16)
-        round_and_deal(nc.vector.tensor_copy, w2_grouped, w2_raw, 1, 16, 64)
-        quantise(w2_codes[:], w2_plane[:], w2_grouped[:].rearrange("p t m j -> p (t m j)"))
 
-        ew_all = tile([P, S], U32, "ew_all", tag="w2_raw1")
-        ew_picked = [ew_all[:, c * CHUNK : (c + 1) * CHUNK] for c in range(CHUNKS)]
+        round_weight(w2_grouped, w2_raw, W2_SCALAR_GROUPS)
+        quantise(w2_codes[:], w2_plane[:], w2_grouped[:].rearrange("p t g j -> p (t g j)"))
 
-        def gather_e(first, last):
-            entries = tok_sb[:, first * LIST_COLS : last * LIST_COLS]
-            picked = ew_all[:, first * CHUNK : last * CHUNK]
-            nc.vector.tensor_copy(picked, ew_table[:].bitcast(U32).indirect(entries))
+        ew_picked = tile([P, S], U32, "ew_picked", tag="w2_raw1")
+
+        def gather_e_words(first, last):
+            nc.vector.tensor_copy(
+                ew_picked[:, columns(first, last)],
+                ew_table[:].bitcast(U32).indirect(entries(tok_sb, first, last)),
+            )
 
         y_codes = tile([P, S], U32, "y_codes")
         y_plane = tile([P, S], U8, "y_plane")
         h_bf = [tile([P, CHUNK, PACK], BF16, "h_bf%d" % c) for c in range(CHUNKS)]
-        y_bf_all = tile([P, S, PACK], BF16, "y_bf")
-        y_bf = [y_bf_all[:, c * CHUNK : (c + 1) * CHUNK, :] for c in range(CHUNKS)]
+        y_bf = tile([P, S, PACK], BF16, "y_bf")
         y_f32 = [tile([P, PACK, CHUNK], F32, "y_f32%d" % c) for c in range(CHUNKS)]
         pre = [psum.tile([P, PACK, CHUNK], F32, name="pre%d" % c) for c in range(CHUNKS)]
 
         def x_pass(c, t):
-            cols = slice(c * CHUNK, (c + 1) * CHUNK)
-            wc = slice(t * P, (t + 1) * P)
+            cols = columns(c, c + 1)
+            places = slice(t * P, (t + 1) * P)
             nc.tensor.matmul_mx(
-                out=pre[c][:, t, :], lhsT=w1_codes[:, wc].bitcast(FP8X4), lhsT_scale=w1_plane[:, wc],
+                out=pre[c][:, t, :], lhsT=w1_codes[:, places].bitcast(FP8X4), lhsT_scale=w1_plane[:, places],
                 rhs=xw_picked[:, cols].bitcast(FP8X4), rhs_scale=xs_picked[:, cols],
                 start=True, stop=False,
             )
 
         def e_pass(c, t):
-            cols = slice(c * CHUNK, (c + 1) * CHUNK)
-            wc = slice(t * P, (t + 1) * P)
+            cols = columns(c, c + 1)
+            places = slice(t * P, (t + 1) * P)
             nc.tensor.matmul_mx(
-                out=pre[c][:, t, :], lhsT=w2_codes[:, wc].bitcast(FP8X4), lhsT_scale=w2_plane[:, wc],
-                rhs=ew_picked[c].bitcast(FP8X4), rhs_scale=es_picked[:, cols],
+                out=pre[c][:, t, :], lhsT=w2_codes[:, places].bitcast(FP8X4), lhsT_scale=w2_plane[:, places],
+                rhs=ew_picked[:, cols].bitcast(FP8X4),
+                rhs_scale=es_late[:] if c == LAST else es_early[:, cols],
                 start=False, stop=True,
             )
 
@@ -170,63 +178,59 @@ def tile_picked_zeagle_silu_po_kernel(
             nc.scalar.activation(out=h_bf[c][:], in_=pre[c][:].rearrange("p t n -> p n t"), func=SILU)
 
         def second_layer(c):
-            cols = slice(c * CHUNK, (c + 1) * CHUNK)
+            cols = columns(c, c + 1)
             h_codes = tile([P, CHUNK], U32, "h_codes%d" % c, tag="h_codes%d" % (c % 2))
             quantise(h_codes[:], h_plane[:, cols], h_bf[c][:].rearrange("p n t -> p (n t)"))
             bank = psum.tile([P, PACK, CHUNK], F32, name="post%d" % c)
             for t in range(PACK):
                 nc.tensor.matmul_mx(
                     out=bank[:, t, :],
-                    lhsT=w3_codes[:, t, :, :].rearrange("p m b -> p (m b)").bitcast(FP4X4),
+                    lhsT=w3_codes[:, t, :, :].rearrange("p g b -> p (g b)").bitcast(FP4X4),
                     lhsT_scale=w3_plane[:, t, :],
                     rhs=h_codes[:].bitcast(FP8X4), rhs_scale=h_plane[:, cols],
                     start=True, stop=True,
                 )
             return bank
 
-        def add_and_store(c, bank):
-            cols = slice(c * CHUNK, (c + 1) * CHUNK)
-            added = skip_sb[0][:] if c == 0 else skip_sb[1][:, :, (c - 1) * CHUNK : c * CHUNK]
+        def add_store_round(c, bank):
+            cols = columns(c, c + 1)
+            added = skip_first[:] if c == 0 else skip_rest[:, :, columns(c - 1, c)]
             nc.vector.tensor_tensor(y_f32[c][:], bank[:], added, ADD)
             nc.sync.dma_start(out=out_0[:, cols].rearrange("(p t) j -> p t j", t=PACK), in_=y_f32[c][:])
-            copy = nc.vector.tensor_copy if c == CHUNKS - 1 else nc.scalar.copy
+            copy = nc.vector.tensor_copy if c == LAST else nc.scalar.copy
             copy(
-                out=y_bf[c].rearrange("p (g i) t -> p g t i", i=4),
-                in_=y_f32[c][:].rearrange("p t (g i) -> p g t i", i=4),
+                out=y_bf[:, cols, :].rearrange("p (a i) t -> p a t i", i=4),
+                in_=y_f32[c][:].rearrange("p t (a i) -> p a t i", i=4),
             )
 
         def quantise_out(first, last):
-            cols = slice(first * CHUNK, last * CHUNK)
-            quantise(y_codes[:, cols], y_plane[:, cols], y_bf_all[:, cols, :].rearrange("p n t -> p (n t)"))
+            cols = columns(first, last)
+            quantise(y_codes[:, cols], y_plane[:, cols], y_bf[:, cols, :].rearrange("p n t -> p (n t)"))
 
         for c in range(CHUNKS):
             x_pass(c, 0)
-        gather_e(0, 1)
-        gather_e(1, 2)
-        gather_e(2, 4)
+        gather_e_words(0, 1)
+        gather_e_words(1, 2)
+        gather_e_words(2, CHUNKS)
+        es_late = tile([P, CHUNK], U8, "es_late", tag="w2_grouped")
+        nc.vector.tensor_copy(es_late[:], es_table[:].indirect(entries(tok_sb, LAST, CHUNKS)))
         first_layer(0)
         w3_plane = tile([P, PACK, P], U8, "w3_plane")
-        nc.vector.tensor_copy(
-            w3_plane[:],
-            w3s_raw[:].rearrange("p (m t) -> p t m", t=PACK),
-        )
+        nc.vector.tensor_copy(w3_plane[:], w3s_raw[:].rearrange("p (g t) -> p t g", t=PACK))
         h_plane = tile([P, S], U8, "h_plane", tag="w3s_raw")
-        first_layer(1)
-        first_layer(2)
-        first_layer(3)
-        banks = [second_layer(c) for c in range(CHUNKS - 1)]
-        add_and_store(0, banks[0])
-        banks.append(second_layer(CHUNKS - 1))
         for c in range(1, CHUNKS):
-            add_and_store(c, banks[c])
+            first_layer(c)
+        banks = [second_layer(c) for c in range(LAST)]
+        add_store_round(0, banks[0])
+        banks.append(second_layer(LAST))
+        for c in range(1, CHUNKS):
+            add_store_round(c, banks[c])
         quantise_out(0, 2)
-        quantise_out(2, 3)
-        quantise_out(3, 4)
-        words = out_1[0].rearrange("p c r -> p (c r)").bitcast(I32)
-        nc.sync.dma_start(out=words, in_=y_codes[:].bitcast(I32))
-        for q in range(4):
-            queue = nc.scalar if q % 2 else nc.sync
-            queue.dma_start(
-                out=out_2[0, q:16:4, :].bitcast(I32),
-                in_=y_plane[q:P:32, :].bitcast(I32),
+        quantise_out(2, LAST)
+        quantise_out(LAST, CHUNKS)
+        nc.sync.dma_start(out=out_1[0].rearrange("p c r -> p (c r)").bitcast(I32), in_=y_codes[:].bitcast(I32))
+        for r in range(PACK):
+            nc.scalar.dma_start(
+                out=out_2[0, r:SCALE_ROWS:PACK, :].bitcast(I32),
+                in_=y_plane[r:P:QUADRANT, :].bitcast(I32),
             )

@@ -28,7 +28,6 @@ HALF = H // 2
 GROUPS = HALF // PACK
 W1_SCALAR_GROUPS = 28
 W2_SCALAR_GROUPS = 22
-WARM_UP_PASSES = 3
 
 
 def tile_picked_zeagle_silu_po_kernel(
@@ -125,14 +124,6 @@ def tile_picked_zeagle_silu_po_kernel(
         es_early = tile([P, LAST * CHUNK], U8, "es_early", tag="w1_raw1")
         nc.vector.tensor_copy(es_early[:], es_table[:].indirect(entries(tok_sb, 0, LAST)))
 
-        warm_bank = psum.tile([P, S], F32, name="post%d" % LAST)
-        for t in range(WARM_UP_PASSES):
-            places = slice(t * P, (t + 1) * P)
-            nc.tensor.matmul_mx(
-                out=warm_bank[:], lhsT=w1_codes[:, places].bitcast(FP8X4), lhsT_scale=w1_plane[:, places],
-                rhs=xw_picked[:].bitcast(FP8X4), rhs_scale=xs_picked[:], start=True, stop=True,
-            )
-
         round_weight(w2_grouped, w2_raw, W2_SCALAR_GROUPS)
         quantise(w2_codes[:], w2_plane[:], w2_grouped[:].rearrange("p t g j -> p (t g j)"))
 
@@ -157,7 +148,7 @@ def tile_picked_zeagle_silu_po_kernel(
             nc.tensor.matmul_mx(
                 out=pre[c][:, t, :], lhsT=w1_codes[:, places].bitcast(FP8X4), lhsT_scale=w1_plane[:, places],
                 rhs=xw_picked[:, cols].bitcast(FP8X4), rhs_scale=xs_picked[:, cols],
-                start=True, stop=False,
+                start=t == 0, stop=False,
             )
 
         def e_pass(c, t):
@@ -167,13 +158,11 @@ def tile_picked_zeagle_silu_po_kernel(
                 out=pre[c][:, t, :], lhsT=w2_codes[:, places].bitcast(FP8X4), lhsT_scale=w2_plane[:, places],
                 rhs=ew_picked[:, cols].bitcast(FP8X4),
                 rhs_scale=es_late[:] if c == LAST else es_early[:, cols],
-                start=False, stop=True,
+                start=False, stop=t == PACK - 1,
             )
 
         def first_layer(c):
             for t in range(PACK):
-                if t > 0:
-                    x_pass(c, t)
                 e_pass(c, t)
             nc.scalar.activation(out=h_bf[c][:], in_=pre[c][:].rearrange("p t n -> p n t"), func=SILU)
 
@@ -207,8 +196,16 @@ def tile_picked_zeagle_silu_po_kernel(
             cols = columns(first, last)
             quantise(y_codes[:, cols], y_plane[:, cols], y_bf[:, cols, :].rearrange("p n t -> p (n t)"))
 
+        def store_words(first, last):
+            cols = columns(first, last)
+            nc.sync.dma_start(
+                out=out_1[0].rearrange("p c r -> p (c r)").bitcast(I32)[:, cols],
+                in_=y_codes[:, cols].bitcast(I32),
+            )
+
         for c in range(CHUNKS):
-            x_pass(c, 0)
+            for t in range(PACK):
+                x_pass(c, t)
         gather_e_words(0, 1)
         gather_e_words(1, 2)
         gather_e_words(2, CHUNKS)
@@ -220,17 +217,19 @@ def tile_picked_zeagle_silu_po_kernel(
         h_plane = tile([P, S], U8, "h_plane", tag="w3s_raw")
         for c in range(1, CHUNKS):
             first_layer(c)
-        banks = [second_layer(c) for c in range(LAST)]
-        add_store_round(0, banks[0])
-        banks.append(second_layer(LAST))
-        for c in range(1, CHUNKS):
+        banks = [second_layer(c) for c in range(2)]
+        for c in range(CHUNKS):
             add_store_round(c, banks[c])
+            if c + 2 < CHUNKS:
+                banks.append(second_layer(c + 2))
         quantise_out(0, 2)
+        store_words(0, 2)
         quantise_out(2, LAST)
         quantise_out(LAST, CHUNKS)
-        nc.sync.dma_start(out=out_1[0].rearrange("p c r -> p (c r)").bitcast(I32), in_=y_codes[:].bitcast(I32))
+        store_words(2, CHUNKS)
         for r in range(PACK):
-            nc.scalar.dma_start(
+            queue = nc.scalar if r < 2 else nc.sync
+            queue.dma_start(
                 out=out_2[0, r:SCALE_ROWS:PACK, :].bitcast(I32),
                 in_=y_plane[r:P:QUADRANT, :].bitcast(I32),
             )

@@ -181,16 +181,22 @@ def tile_picked_zeagle_silu_po_kernel(
                 )
             return bank
 
+        def round_out(copy, c, first, last):
+            copy(
+                out=y_bf[:, c * CHUNK + first : c * CHUNK + last, :].rearrange("p (a i) t -> p a t i", i=4),
+                in_=y_f32[c][:, :, first:last].rearrange("p t (a i) -> p a t i", i=4),
+            )
+
         def add_store_round(c, bank):
             cols = columns(c, c + 1)
             added = skip_first[:] if c == 0 else skip_rest[:, :, columns(c - 1, c)]
             nc.vector.tensor_tensor(y_f32[c][:], bank[:], added, ADD)
             nc.sync.dma_start(out=out_0[:, cols].rearrange("(p t) j -> p t j", t=PACK), in_=y_f32[c][:])
-            copy = nc.vector.tensor_copy if c == LAST else nc.scalar.copy
-            copy(
-                out=y_bf[:, cols, :].rearrange("p (a i) t -> p a t i", i=4),
-                in_=y_f32[c][:].rearrange("p t (a i) -> p a t i", i=4),
-            )
+            if c == LAST:
+                round_out(nc.scalar.copy, c, 0, CHUNK // 2)
+                round_out(nc.vector.tensor_copy, c, CHUNK // 2, CHUNK)
+            else:
+                round_out(nc.scalar.copy, c, 0, CHUNK)
 
         def quantise_out(first, last):
             cols = columns(first, last)
@@ -217,11 +223,11 @@ def tile_picked_zeagle_silu_po_kernel(
         h_plane = tile([P, S], U8, "h_plane", tag="w3s_raw")
         for c in range(1, CHUNKS):
             first_layer(c)
-        banks = [second_layer(c) for c in range(2)]
-        for c in range(CHUNKS):
+        banks = [second_layer(c) for c in range(LAST)]
+        add_store_round(0, banks[0])
+        banks.append(second_layer(LAST))
+        for c in range(1, CHUNKS):
             add_store_round(c, banks[c])
-            if c + 2 < CHUNKS:
-                banks.append(second_layer(c + 2))
         quantise_out(0, 2)
         store_words(0, 2)
         quantise_out(2, LAST)

@@ -202,13 +202,6 @@ def tile_picked_zeagle_silu_po_kernel(
             cols = columns(first, last)
             quantise(y_codes[:, cols], y_plane[:, cols], y_bf[:, cols, :].rearrange("p n t -> p (n t)"))
 
-        def store_words(first, last):
-            cols = columns(first, last)
-            nc.sync.dma_start(
-                out=out_1[0].rearrange("p c r -> p (c r)").bitcast(I32)[:, cols],
-                in_=y_codes[:, cols].bitcast(I32),
-            )
-
         for c in range(CHUNKS):
             for t in range(PACK):
                 x_pass(c, t)
@@ -229,13 +222,11 @@ def tile_picked_zeagle_silu_po_kernel(
         for c in range(1, CHUNKS):
             add_store_round(c, banks[c])
         quantise_out(0, 2)
-        store_words(0, 2)
         quantise_out(2, LAST)
         quantise_out(LAST, CHUNKS)
-        store_words(2, CHUNKS)
+        nc.sync.dma_start(out=out_1[0].rearrange("p c r -> p (c r)").bitcast(I32), in_=y_codes[:].bitcast(I32))
         for r in range(PACK):
-            queue = nc.scalar if r < 2 else nc.sync
-            queue.dma_start(
+            nc.scalar.dma_start(
                 out=out_2[0, r:SCALE_ROWS:PACK, :].bitcast(I32),
                 in_=y_plane[r:P:QUADRANT, :].bitcast(I32),
             )

@@ -40,7 +40,7 @@ def tile_picked_zeagle_silu_po_kernel(
         psum = ctx.enter_context(tc.psum_pool(name="psum", bufs=1))
 
         def tile(shape, dtype, name, tag=None):
-            return keep.tile(shape, dtype, name=name, tag=tag or name, align_bytes=64)
+            return keep.tile(shape, dtype, name=name, tag=tag or name, align_bytes=256)
 
         def columns(first, last):
             return slice(first * CHUNK, last * CHUNK)

@@ -68,17 +68,21 @@ def tile_picked_zeagle_silu_po_kernel(
             nc.sync.dma_start(out=table[:], in_=words[0].rearrange("p c r -> p (c r)").bitcast(I32))
             return table
 
-        offs_sb = keep.tile([P, S // 16], U16, name="offs_sb")
-        tok_sb = keep.tile([P, S // 16], U16, name="tok_sb")
+        offs_sb = tile([P, S // 16], U16, "offs_sb")
+        tok_sb = tile([P, S // 16], U16, "tok_sb")
         xs_table = tile([P, T], U8, "xs_table")
         es_table = tile([P, T], U8, "es_table")
         w3s_raw = tile([P, N], U8, "w3s_raw")
 
-        for plane in (xs_table, es_table, w3s_raw):
+        nc.vector.memset(xs_table[:].bitcast(I32), 0)
+        for plane in (es_table, w3s_raw):
             nc.gpsimd.memset(plane[:].bitcast(I32), 0)
 
-        w3w_raw = tile([P, 2 * N], U8, "w3w_raw")
-        nc.sync.dma_start(out=w3w_raw[:].bitcast(I32), in_=w3_words[0].bitcast(I32))
+        warm_in = tile([P, 8], F32, "warm_in")
+        warm_out = tile([P, 8], F32, "warm_out")
+        nc.gpsimd.memset(warm_in[:], 0.0)
+        nc.scalar.activation(out=warm_out[:], in_=warm_in[:], func=SILU)
+
         nc.sync.dma_start(offs_sb[:], offs)
         xw_table = load_words(x_words, "xw_table")
         load_scale_rows(xs_table, x_scales)
@@ -87,9 +91,10 @@ def tile_picked_zeagle_silu_po_kernel(
         load_scale_rows(es_table, e_scales)
         w2_raw = load_halves(w2, "w2_raw")
         ew_table = load_words(e_words, "ew_table")
-        skip_first = load_rows(skip, columns(0, 1), "skip_first")
+        w3w_raw = tile([P, 2 * N], U8, "w3w_raw")
+        nc.sync.dma_start(out=w3w_raw[:].bitcast(I32), in_=w3_words[0].bitcast(I32))
         load_scale_rows(w3s_raw, w3_scales)
-        skip_rest = load_rows(skip, columns(1, CHUNKS), "skip_rest")
+        skip_raw = load_halves(skip, "skip_raw")
 
         def round_and_deal(copy, grouped, raw, half, first, last):
             g0 = half * GROUPS
@@ -114,7 +119,6 @@ def tile_picked_zeagle_silu_po_kernel(
         w2_plane = tile([P, H], U8, "w2_plane")
         w3_codes = tile([P, PACK, P, 2], U8, "w3_codes")
 
-        nc.vector.tensor_copy(w3_codes[:], w3w_raw[:].rearrange("p (g t b) -> p t g b", t=PACK, b=2))
         xw_picked = tile([P, S], U32, "xw_picked")
         nc.vector.tensor_copy(xw_picked[:], xw_table[:].bitcast(U32).indirect(offs_sb[:]))
         nc.vector.tensor_copy(xs_picked[:], xs_table[:].indirect(offs_sb[:]))
@@ -189,7 +193,7 @@ def tile_picked_zeagle_silu_po_kernel(
 
         def add_store_round(c, bank):
             cols = columns(c, c + 1)
-            added = skip_first[:] if c == 0 else skip_rest[:, :, columns(c - 1, c)]
+            added = skip_raw[c // 2][:, :, columns(c % 2, c % 2 + 1)]
             nc.vector.tensor_tensor(y_f32[c][:], bank[:], added, ADD)
             nc.sync.dma_start(out=out_0[:, cols].rearrange("(p t) j -> p t j", t=PACK), in_=y_f32[c][:])
             if c == LAST:
@@ -210,15 +214,19 @@ def tile_picked_zeagle_silu_po_kernel(
         gather_e_words(2, CHUNKS)
         es_late = tile([P, CHUNK], U8, "es_late", tag="w2_grouped")
         nc.vector.tensor_copy(es_late[:], es_table[:].indirect(entries(tok_sb, LAST, CHUNKS)))
+        nc.scalar.copy(
+            out=w3_codes[:].rearrange("p t g b -> p (t g b)").bitcast(U16).rearrange("p (t g) -> p t g", t=PACK),
+            in_=w3w_raw[:].bitcast(U16).rearrange("p (g t) -> p t g", t=PACK),
+        )
         first_layer(0)
         w3_plane = tile([P, PACK, P], U8, "w3_plane")
         nc.vector.tensor_copy(w3_plane[:], w3s_raw[:].rearrange("p (g t) -> p t g", t=PACK))
         h_plane = tile([P, S], U8, "h_plane", tag="w3s_raw")
         for c in range(1, CHUNKS):
             first_layer(c)
-        banks = [second_layer(c) for c in range(LAST)]
+        banks = [second_layer(c) for c in range(2)]
         add_store_round(0, banks[0])
-        banks.append(second_layer(LAST))
+        banks.extend(second_layer(c) for c in range(2, CHUNKS))
         for c in range(1, CHUNKS):
             add_store_round(c, banks[c])
         quantise_out(0, 2)

@@ -27,7 +27,7 @@ LIST_COLS = CHUNK // 16
 HALF = H // 2
 GROUPS = HALF // PACK
 W1_SCALAR_GROUPS = 28
-W2_SCALAR_GROUPS = 22
+W2_SCALAR_GROUPS = 28
 
 
 def tile_picked_zeagle_silu_po_kernel(
@@ -60,8 +60,8 @@ def tile_picked_zeagle_silu_po_kernel(
             nc.sync.dma_start(out=raw[:], in_=matrix[:, cols].rearrange("(p j) c -> p j c", j=PACK))
             return raw
 
-        def load_halves(w, name):
-            return [load_rows(w, slice(half * HALF, (half + 1) * HALF), name + str(half)) for half in range(2)]
+        def load_half(w, name, half):
+            return load_rows(w, slice(half * HALF, (half + 1) * HALF), name + str(half))
 
         def load_words(words, name):
             table = tile([P, T], I32, name)
@@ -83,24 +83,26 @@ def tile_picked_zeagle_silu_po_kernel(
         nc.gpsimd.memset(warm_in[:], 0.0)
         nc.scalar.activation(out=warm_out[:], in_=warm_in[:], func=SILU)
 
-        nc.sync.dma_start(offs_sb[:], offs)
         xw_table = load_words(x_words, "xw_table")
+        nc.sync.dma_start(offs_sb[:], offs)
+        w1_raw = [load_half(w1, "w1_raw", 0)]
         load_scale_rows(xs_table, x_scales)
-        w1_raw = load_halves(w1, "w1_raw")
+        w1_raw.append(load_half(w1, "w1_raw", 1))
+        w2_raw = [load_half(w2, "w2_raw", 0)]
         nc.sync.dma_start(tok_sb[:], tok)
         load_scale_rows(es_table, e_scales)
-        w2_raw = load_halves(w2, "w2_raw")
+        w2_raw.append(load_half(w2, "w2_raw", 1))
         ew_table = load_words(e_words, "ew_table")
         w3w_raw = tile([P, 2 * N], U8, "w3w_raw")
         nc.sync.dma_start(out=w3w_raw[:].bitcast(I32), in_=w3_words[0].bitcast(I32))
         load_scale_rows(w3s_raw, w3_scales)
-        skip_raw = load_halves(skip, "skip_raw")
+        skip_raw = [load_half(skip, "skip_raw", half) for half in range(2)]
 
         def round_and_deal(copy, grouped, raw, half, first, last):
             g0 = half * GROUPS
             copy(
-                out=grouped[:, :, g0 + first : g0 + last, :].rearrange("p t g j -> p g j t"),
-                in_=raw[half][:].rearrange("p j (g t) -> p g j t", t=PACK)[:, first:last, :, :],
+                out=grouped[:, :, g0 + first : g0 + last, :].rearrange("p (u v) g j -> p u g j v", v=2),
+                in_=raw[half][:].rearrange("p j (g u v) -> p u g j v", u=2, v=2)[:, :, first:last, :, :],
             )
 
         def round_weight(grouped, raw, scalar_groups):

@@ -95,8 +95,9 @@ def tile_picked_zeagle_silu_po_kernel(
         ew_table = load_words(e_words, "ew_table")
         w3w_raw = tile([P, 2 * N], U8, "w3w_raw")
         nc.sync.dma_start(out=w3w_raw[:].bitcast(I32), in_=w3_words[0].bitcast(I32))
+        skip_first = load_rows(skip, columns(0, 1), "skip_first")
         load_scale_rows(w3s_raw, w3_scales)
-        skip_raw = [load_half(skip, "skip_raw", half) for half in range(2)]
+        skip_rest = load_rows(skip, columns(1, CHUNKS), "skip_rest")
 
         def round_and_deal(copy, grouped, raw, half, first, last):
             g0 = half * GROUPS
@@ -176,16 +177,23 @@ def tile_picked_zeagle_silu_po_kernel(
             cols = columns(c, c + 1)
             h_codes = tile([P, CHUNK], U32, "h_codes%d" % c, tag="h_codes%d" % (c % 2))
             quantise(h_codes[:], h_plane[:, cols], h_bf[c][:].rearrange("p n t -> p (n t)"))
-            bank = psum.tile([P, PACK, CHUNK], F32, name="post%d" % c)
+            if c == 0:
+                parts = [
+                    psum.tile([P, 2, CHUNK], F32, name="post0"),
+                    psum.tile([P, 2, CHUNK], F32, name="post0b", tag="pre0"),
+                ]
+            else:
+                parts = [psum.tile([P, PACK, CHUNK], F32, name="post%d" % c)]
+            width = PACK // len(parts)
             for t in range(PACK):
                 nc.tensor.matmul_mx(
-                    out=bank[:, t, :],
+                    out=parts[t // width][:, t % width, :],
                     lhsT=w3_codes[:, t, :, :].rearrange("p g b -> p (g b)").bitcast(FP4X4),
                     lhsT_scale=w3_plane[:, t, :],
                     rhs=h_codes[:].bitcast(FP8X4), rhs_scale=h_plane[:, cols],
                     start=True, stop=True,
                 )
-            return bank
+            return parts
 
         def round_out(copy, c, first, last):
             copy(
@@ -193,10 +201,13 @@ def tile_picked_zeagle_silu_po_kernel(
                 in_=y_f32[c][:, :, first:last].rearrange("p t (a i) -> p a t i", i=4),
             )
 
-        def add_store_round(c, bank):
+        def add_store_round(c, parts):
             cols = columns(c, c + 1)
-            added = skip_raw[c // 2][:, :, columns(c % 2, c % 2 + 1)]
-            nc.vector.tensor_tensor(y_f32[c][:], bank[:], added, ADD)
+            added = skip_first[:] if c == 0 else skip_rest[:, :, columns(c - 1, c)]
+            width = PACK // len(parts)
+            for i, part in enumerate(parts):
+                rows = slice(i * width, (i + 1) * width)
+                nc.vector.tensor_tensor(y_f32[c][:, rows, :], part[:], added[:, rows, :], ADD)
             nc.sync.dma_start(out=out_0[:, cols].rearrange("(p t) j -> p t j", t=PACK), in_=y_f32[c][:])
             if c == LAST:
                 round_out(nc.scalar.copy, c, 0, CHUNK // 2)

@@ -28,6 +28,8 @@ HALF = H // 2
 GROUPS = HALF // PACK
 W1_SCALAR_GROUPS = 28
 W2_SCALAR_GROUPS = 28
+X_ROW = 4
+E_ROW = 8
 
 
 def tile_picked_zeagle_silu_po_kernel(
@@ -48,10 +50,10 @@ def tile_picked_zeagle_silu_po_kernel(
         def entries(list_tile, first, last):
             return list_tile[:, first * LIST_COLS : last * LIST_COLS]
 
-        def load_scale_rows(plane, rows):
+        def load_scale_rows(plane, rows, first_row=0):
             for r in range(PACK):
                 nc.sync.dma_start(
-                    out=plane[r:P:QUADRANT, :].bitcast(I32),
+                    out=plane[first_row + r : P : QUADRANT, :].bitcast(I32),
                     in_=rows[0, r:SCALE_ROWS:PACK, :].bitcast(I32),
                 )
 
@@ -86,11 +88,11 @@ def tile_picked_zeagle_silu_po_kernel(
         xw_table = load_words(x_words, "xw_table")
         nc.sync.dma_start(offs_sb[:], offs)
         w1_raw = [load_half(w1, "w1_raw", 0)]
-        load_scale_rows(xs_table, x_scales)
+        load_scale_rows(xs_table, x_scales, X_ROW)
         w1_raw.append(load_half(w1, "w1_raw", 1))
         w2_raw = [load_half(w2, "w2_raw", 0)]
         nc.sync.dma_start(tok_sb[:], tok)
-        load_scale_rows(es_table, e_scales)
+        load_scale_rows(es_table, e_scales, E_ROW)
         w2_raw.append(load_half(w2, "w2_raw", 1))
         ew_table = load_words(e_words, "ew_table")
         w3w_raw = tile([P, 2 * N], U8, "w3w_raw")
@@ -154,7 +156,7 @@ def tile_picked_zeagle_silu_po_kernel(
             places = slice(t * P, (t + 1) * P)
             nc.tensor.matmul_mx(
                 out=pre[c][:, t, :], lhsT=w1_codes[:, places].bitcast(FP8X4), lhsT_scale=w1_plane[:, places],
-                rhs=xw_picked[:, cols].bitcast(FP8X4), rhs_scale=xs_picked[:, cols],
+                rhs=xw_picked[:, cols].bitcast(FP8X4), rhs_scale=xs_picked[X_ROW:P, cols],
                 start=t == 0, stop=False,
             )
 
@@ -164,7 +166,7 @@ def tile_picked_zeagle_silu_po_kernel(
             nc.tensor.matmul_mx(
                 out=pre[c][:, t, :], lhsT=w2_codes[:, places].bitcast(FP8X4), lhsT_scale=w2_plane[:, places],
                 rhs=ew_picked[:, cols].bitcast(FP8X4),
-                rhs_scale=es_late[:] if c == LAST else es_early[:, cols],
+                rhs_scale=es_late[E_ROW:P, :] if c == LAST else es_early[E_ROW:P, cols],
                 start=False, stop=t == PACK - 1,
             )
 

@@ -97,9 +97,9 @@ def tile_picked_zeagle_silu_po_kernel(
         ew_table = load_words(e_words, "ew_table")
         w3w_raw = tile([P, 2 * N], U8, "w3w_raw")
         nc.sync.dma_start(out=w3w_raw[:].bitcast(I32), in_=w3_words[0].bitcast(I32))
-        skip_first = load_rows(skip, columns(0, 1), "skip_first")
+        skip_first = load_rows(skip, columns(0, 2), "skip_first")
         load_scale_rows(w3s_raw, w3_scales)
-        skip_rest = load_rows(skip, columns(1, CHUNKS), "skip_rest")
+        skip_rest = load_rows(skip, columns(2, CHUNKS), "skip_rest")
 
         def round_and_deal(copy, grouped, raw, half, first, last):
             g0 = half * GROUPS
@@ -179,10 +179,10 @@ def tile_picked_zeagle_silu_po_kernel(
             cols = columns(c, c + 1)
             h_codes = tile([P, CHUNK], U32, "h_codes%d" % c, tag="h_codes%d" % (c % 2))
             quantise(h_codes[:], h_plane[:, cols], h_bf[c][:].rearrange("p n t -> p (n t)"))
-            if c == 0:
+            if c in (0, LAST):
                 parts = [
-                    psum.tile([P, 2, CHUNK], F32, name="post0"),
-                    psum.tile([P, 2, CHUNK], F32, name="post0b", tag="pre0"),
+                    psum.tile([P, 2, CHUNK], F32, name="post%d" % c),
+                    psum.tile([P, 2, CHUNK], F32, name="post%db" % c, tag="pre%d" % min(c, 1)),
                 ]
             else:
                 parts = [psum.tile([P, PACK, CHUNK], F32, name="post%d" % c)]
@@ -203,13 +203,17 @@ def tile_picked_zeagle_silu_po_kernel(
                 in_=y_f32[c][:, :, first:last].rearrange("p t (a i) -> p a t i", i=4),
             )
 
-        def add_store_round(c, parts):
+        def add_half(c, parts, i):
+            added = skip_first[:, :, columns(c, c + 1)] if c < 2 else skip_rest[:, :, columns(c - 2, c - 1)]
+            rows = slice(2 * i, 2 * i + 2)
+            part = parts[i][:] if len(parts) == 2 else parts[0][:, rows, :]
+            nc.vector.tensor_tensor(y_f32[c][:, rows, :], part, added[:, rows, :], ADD)
+
+        def add_whole(c, parts):
+            nc.vector.tensor_tensor(y_f32[c][:], parts[0][:], skip_rest[:, :, columns(c - 2, c - 1)], ADD)
+
+        def store_round(c):
             cols = columns(c, c + 1)
-            added = skip_first[:] if c == 0 else skip_rest[:, :, columns(c - 1, c)]
-            width = PACK // len(parts)
-            for i, part in enumerate(parts):
-                rows = slice(i * width, (i + 1) * width)
-                nc.vector.tensor_tensor(y_f32[c][:, rows, :], part[:], added[:, rows, :], ADD)
             nc.sync.dma_start(out=out_0[:, cols].rearrange("(p t) j -> p t j", t=PACK), in_=y_f32[c][:])
             if c == LAST:
                 round_out(nc.scalar.copy, c, 0, CHUNK // 2)
@@ -235,15 +239,24 @@ def tile_picked_zeagle_silu_po_kernel(
         )
         first_layer(0)
         w3_plane = tile([P, PACK, P], U8, "w3_plane")
-        nc.vector.tensor_copy(w3_plane[:], w3s_raw[:].rearrange("p (g t) -> p t g", t=PACK))
-        h_plane = tile([P, S], U8, "h_plane", tag="w3s_raw")
+        nc.gpsimd.tensor_copy(w3_plane[:], w3s_raw[:].rearrange("p (g t) -> p t g", t=PACK))
+        h_plane = tile([P, S], U8, "h_plane")
         for c in range(1, CHUNKS):
             first_layer(c)
         banks = [second_layer(c) for c in range(2)]
-        add_store_round(0, banks[0])
-        banks.extend(second_layer(c) for c in range(2, CHUNKS))
-        for c in range(1, CHUNKS):
-            add_store_round(c, banks[c])
+        add_half(0, banks[0], 0)
+        add_half(0, banks[0], 1)
+        store_round(0)
+        banks.append(second_layer(2))
+        add_half(1, banks[1], 0)
+        banks.append(second_layer(LAST))
+        add_half(1, banks[1], 1)
+        store_round(1)
+        add_whole(2, banks[2])
+        store_round(2)
+        add_half(LAST, banks[LAST], 0)
+        add_half(LAST, banks[LAST], 1)
+        store_round(LAST)
         quantise_out(0, 2)
         quantise_out(2, LAST)
         quantise_out(LAST, CHUNKS)

@@ -24,10 +24,9 @@ CHUNK = 128
 CHUNKS = S // CHUNK
 LAST = CHUNKS - 1
 LIST_COLS = CHUNK // 16
+SKIP_SPLIT = CHUNK + CHUNK // 2
 HALF = H // 2
 GROUPS = HALF // PACK
-W1_SCALAR_GROUPS = 28
-W2_SCALAR_GROUPS = 28
 X_ROW = 4
 E_ROW = 8
 
@@ -97,9 +96,9 @@ def tile_picked_zeagle_silu_po_kernel(
         ew_table = load_words(e_words, "ew_table")
         w3w_raw = tile([P, 2 * N], U8, "w3w_raw")
         nc.sync.dma_start(out=w3w_raw[:].bitcast(I32), in_=w3_words[0].bitcast(I32))
-        skip_first = load_rows(skip, columns(0, 2), "skip_first")
+        skip_first = load_rows(skip, slice(0, SKIP_SPLIT), "skip_first")
         load_scale_rows(w3s_raw, w3_scales)
-        skip_rest = load_rows(skip, columns(2, CHUNKS), "skip_rest")
+        skip_rest = load_rows(skip, slice(SKIP_SPLIT, S), "skip_rest")
 
         def round_and_deal(copy, grouped, raw, half, first, last):
             g0 = half * GROUPS
@@ -108,10 +107,21 @@ def tile_picked_zeagle_silu_po_kernel(
                 in_=raw[half][:].rearrange("p j (g u v) -> p u g j v", u=2, v=2)[:, :, first:last, :, :],
             )
 
-        def round_weight(grouped, raw, scalar_groups):
+        def round_pair(copy, grouped, raw, u):
+            copy(
+                out=grouped[:, 2 * u : 2 * u + 2, GROUPS:, :].rearrange("p v g j -> p g j v"),
+                in_=raw[1][:].rearrange("p j (g t) -> p g j t", t=PACK)[:, :, :, 2 * u : 2 * u + 2],
+            )
+
+        def round_weight(grouped, raw):
             round_and_deal(nc.scalar.copy, grouped, raw, 0, 0, GROUPS)
-            round_and_deal(nc.scalar.copy, grouped, raw, 1, 0, scalar_groups)
-            round_and_deal(nc.vector.tensor_copy, grouped, raw, 1, scalar_groups, GROUPS)
+            round_pair(nc.vector.tensor_copy, grouped, raw, 0)
+            round_pair(nc.scalar.copy, grouped, raw, 1)
+
+        def quantise_weight(codes, plane, grouped):
+            for u in range(2):
+                places = slice(2 * u * P, (2 * u + 2) * P)
+                quantise(codes[:, places], plane[:, places], grouped[:, 2 * u : 2 * u + 2, :, :].rearrange("p t g j -> p (t g j)"))
 
         def quantise(codes, plane, values):
             nc.vector.quantize_mx(out=codes.bitcast(FP8X4), scales=plane, in_=values)
@@ -127,14 +137,14 @@ def tile_picked_zeagle_silu_po_kernel(
         xw_picked = tile([P, S], U32, "xw_picked")
         nc.vector.tensor_copy(xw_picked[:], xw_table[:].bitcast(U32).indirect(offs_sb[:]))
         nc.vector.tensor_copy(xs_picked[:], xs_table[:].indirect(offs_sb[:]))
-        round_weight(w1_grouped, w1_raw, W1_SCALAR_GROUPS)
+        round_weight(w1_grouped, w1_raw)
         w1_plane = tile([P, H], U8, "w1_plane")
-        quantise(w1_codes[:], w1_plane[:], w1_grouped[:].rearrange("p t g j -> p (t g j)"))
+        quantise_weight(w1_codes, w1_plane, w1_grouped)
         es_early = tile([P, LAST * CHUNK], U8, "es_early", tag="w1_raw1")
         nc.vector.tensor_copy(es_early[:], es_table[:].indirect(entries(tok_sb, 0, LAST)))
 
-        round_weight(w2_grouped, w2_raw, W2_SCALAR_GROUPS)
-        quantise(w2_codes[:], w2_plane[:], w2_grouped[:].rearrange("p t g j -> p (t g j)"))
+        round_weight(w2_grouped, w2_raw)
+        quantise_weight(w2_codes, w2_plane, w2_grouped)
 
         ew_picked = tile([P, S], U32, "ew_picked", tag="w2_raw1")
 
@@ -179,7 +189,7 @@ def tile_picked_zeagle_silu_po_kernel(
             cols = columns(c, c + 1)
             h_codes = tile([P, CHUNK], U32, "h_codes%d" % c, tag="h_codes%d" % (c % 2))
             quantise(h_codes[:], h_plane[:, cols], h_bf[c][:].rearrange("p n t -> p (n t)"))
-            if c in (0, LAST):
+            if c == 0:
                 parts = [
                     psum.tile([P, 2, CHUNK], F32, name="post%d" % c),
                     psum.tile([P, 2, CHUNK], F32, name="post%db" % c, tag="pre%d" % min(c, 1)),
@@ -203,14 +213,13 @@ def tile_picked_zeagle_silu_po_kernel(
                 in_=y_f32[c][:, :, first:last].rearrange("p t (a i) -> p a t i", i=4),
             )
 
-        def add_half(c, parts, i):
-            added = skip_first[:, :, columns(c, c + 1)] if c < 2 else skip_rest[:, :, columns(c - 2, c - 1)]
-            rows = slice(2 * i, 2 * i + 2)
-            part = parts[i][:] if len(parts) == 2 else parts[0][:, rows, :]
-            nc.vector.tensor_tensor(y_f32[c][:, rows, :], part, added[:, rows, :], ADD)
-
-        def add_whole(c, parts):
-            nc.vector.tensor_tensor(y_f32[c][:], parts[0][:], skip_rest[:, :, columns(c - 2, c - 1)], ADD)
+        def add_skip(c, part, rows, first, last):
+            start, stop = c * CHUNK + first, c * CHUNK + last
+            if stop <= SKIP_SPLIT:
+                added = skip_first[:, rows, start:stop]
+            else:
+                added = skip_rest[:, rows, start - SKIP_SPLIT : stop - SKIP_SPLIT]
+            nc.vector.tensor_tensor(y_f32[c][:, rows, first:last], part[:, :, first:last], added, ADD)
 
         def store_round(c):
             cols = columns(c, c + 1)
@@ -225,38 +234,38 @@ def tile_picked_zeagle_silu_po_kernel(
             cols = columns(first, last)
             quantise(y_codes[:, cols], y_plane[:, cols], y_bf[:, cols, :].rearrange("p n t -> p (n t)"))
 
-        for c in range(CHUNKS):
-            for t in range(PACK):
-                x_pass(c, t)
+        for u in range(2):
+            for c in range(CHUNKS):
+                x_pass(c, 2 * u)
+                x_pass(c, 2 * u + 1)
         gather_e_words(0, 1)
         gather_e_words(1, 2)
         gather_e_words(2, CHUNKS)
-        es_late = tile([P, CHUNK], U8, "es_late", tag="w2_grouped")
-        nc.vector.tensor_copy(es_late[:], es_table[:].indirect(entries(tok_sb, LAST, CHUNKS)))
         nc.scalar.copy(
             out=w3_codes[:].rearrange("p t g b -> p (t g b)").bitcast(U16).rearrange("p (t g) -> p t g", t=PACK),
             in_=w3w_raw[:].bitcast(U16).rearrange("p (g t) -> p t g", t=PACK),
         )
+        es_late = tile([P, CHUNK], U8, "es_late", tag="w3w_raw")
+        nc.vector.tensor_copy(es_late[:], es_table[:].indirect(entries(tok_sb, LAST, CHUNKS)))
         first_layer(0)
         w3_plane = tile([P, PACK, P], U8, "w3_plane")
         nc.gpsimd.tensor_copy(w3_plane[:], w3s_raw[:].rearrange("p (g t) -> p t g", t=PACK))
         h_plane = tile([P, S], U8, "h_plane")
         for c in range(1, CHUNKS):
             first_layer(c)
+        every_row = slice(0, PACK)
         banks = [second_layer(c) for c in range(2)]
-        add_half(0, banks[0], 0)
-        add_half(0, banks[0], 1)
+        add_skip(0, banks[0][0], slice(0, 2), 0, CHUNK)
+        add_skip(0, banks[0][1], slice(2, PACK), 0, CHUNK)
         store_round(0)
         banks.append(second_layer(2))
-        add_half(1, banks[1], 0)
+        add_skip(1, banks[1][0], every_row, 0, CHUNK // 2)
         banks.append(second_layer(LAST))
-        add_half(1, banks[1], 1)
+        add_skip(1, banks[1][0], every_row, CHUNK // 2, CHUNK)
         store_round(1)
-        add_whole(2, banks[2])
-        store_round(2)
-        add_half(LAST, banks[LAST], 0)
-        add_half(LAST, banks[LAST], 1)
-        store_round(LAST)
+        for c in range(2, CHUNKS):
+            add_skip(c, banks[c][0], every_row, 0, CHUNK)
+            store_round(c)
         quantise_out(0, 2)
         quantise_out(2, LAST)
         quantise_out(LAST, CHUNKS)

@@ -25,6 +25,7 @@ CHUNKS = S // CHUNK
 LAST = CHUNKS - 1
 LIST_COLS = CHUNK // 16
 SKIP_SPLIT = CHUNK + CHUNK // 2
+VECTOR_GROUPS = 50
 HALF = H // 2
 GROUPS = HALF // PACK
 X_ROW = 4
@@ -107,15 +108,16 @@ def tile_picked_zeagle_silu_po_kernel(
                 in_=raw[half][:].rearrange("p j (g u v) -> p u g j v", u=2, v=2)[:, :, first:last, :, :],
             )
 
-        def round_pair(copy, grouped, raw, u):
+        def round_pair(copy, grouped, raw, u, first=0, last=GROUPS):
             copy(
-                out=grouped[:, 2 * u : 2 * u + 2, GROUPS:, :].rearrange("p v g j -> p g j v"),
-                in_=raw[1][:].rearrange("p j (g t) -> p g j t", t=PACK)[:, :, :, 2 * u : 2 * u + 2],
+                out=grouped[:, 2 * u : 2 * u + 2, GROUPS + first : GROUPS + last, :].rearrange("p v g j -> p g j v"),
+                in_=raw[1][:].rearrange("p j (g t) -> p g j t", t=PACK)[:, first:last, :, 2 * u : 2 * u + 2],
             )
 
         def round_weight(grouped, raw):
             round_and_deal(nc.scalar.copy, grouped, raw, 0, 0, GROUPS)
-            round_pair(nc.vector.tensor_copy, grouped, raw, 0)
+            round_pair(nc.vector.tensor_copy, grouped, raw, 0, 0, VECTOR_GROUPS)
+            round_pair(nc.scalar.copy, grouped, raw, 0, VECTOR_GROUPS, GROUPS)
             round_pair(nc.scalar.copy, grouped, raw, 1)
 
         def quantise_weight(codes, plane, grouped):

@@ -97,8 +97,8 @@ def tile_picked_zeagle_silu_po_kernel(
         ew_table = load_words(e_words, "ew_table")
         w3w_raw = tile([P, 2 * N], U8, "w3w_raw")
         nc.sync.dma_start(out=w3w_raw[:].bitcast(I32), in_=w3_words[0].bitcast(I32))
-        skip_first = load_rows(skip, slice(0, SKIP_SPLIT), "skip_first")
         load_scale_rows(w3s_raw, w3_scales)
+        skip_first = load_rows(skip, slice(0, SKIP_SPLIT), "skip_first")
         skip_rest = load_rows(skip, slice(SKIP_SPLIT, S), "skip_rest")
 
         def round_and_deal(copy, grouped, raw, half, first, last):
@@ -182,15 +182,24 @@ def tile_picked_zeagle_silu_po_kernel(
                 start=False, stop=t == PACK - 1,
             )
 
+        def pieces(c):
+            width = CHUNK // 2 if c == 0 else CHUNK
+            return [slice(n, n + width) for n in range(0, CHUNK, width)]
+
         def first_layer(c):
             for t in range(PACK):
                 e_pass(c, t)
-            nc.scalar.activation(out=h_bf[c][:], in_=pre[c][:].rearrange("p t n -> p n t"), func=SILU)
+            for part in pieces(c):
+                nc.scalar.activation(
+                    out=h_bf[c][:, part, :], in_=pre[c][:, :, part].rearrange("p t n -> p n t"), func=SILU
+                )
 
         def second_layer(c):
             cols = columns(c, c + 1)
             h_codes = tile([P, CHUNK], U32, "h_codes%d" % c, tag="h_codes%d" % (c % 2))
-            quantise(h_codes[:], h_plane[:, cols], h_bf[c][:].rearrange("p n t -> p (n t)"))
+            for part in pieces(c):
+                place = slice(cols.start + part.start, cols.start + part.stop)
+                quantise(h_codes[:, part], h_plane[:, place], h_bf[c][:, part, :].rearrange("p n t -> p (n t)"))
             if c == 0:
                 parts = [
                     psum.tile([P, 2, CHUNK], F32, name="post%d" % c),

@@ -232,14 +232,13 @@ def tile_picked_zeagle_silu_po_kernel(
                 added = skip_rest[:, rows, start - SKIP_SPLIT : stop - SKIP_SPLIT]
             nc.vector.tensor_tensor(y_f32[c][:, rows, first:last], part[:, :, first:last], added, ADD)
 
-        def store_round(c):
+        def store(c):
             cols = columns(c, c + 1)
             nc.sync.dma_start(out=out_0[:, cols].rearrange("(p t) j -> p t j", t=PACK), in_=y_f32[c][:])
-            if c == LAST:
-                round_out(nc.scalar.copy, c, 0, CHUNK // 2)
-                round_out(nc.vector.tensor_copy, c, CHUNK // 2, CHUNK)
-            else:
-                round_out(nc.scalar.copy, c, 0, CHUNK)
+
+        def add_and_round(c, first, last, copy):
+            add_skip(c, banks[c][0], slice(0, PACK), first, last)
+            round_out(copy, c, first, last)
 
         def quantise_out(first, last):
             cols = columns(first, last)
@@ -264,19 +263,25 @@ def tile_picked_zeagle_silu_po_kernel(
         h_plane = tile([P, S], U8, "h_plane")
         for c in range(1, CHUNKS):
             first_layer(c)
-        every_row = slice(0, PACK)
         banks = [second_layer(c) for c in range(2)]
         add_skip(0, banks[0][0], slice(0, 2), 0, CHUNK)
         add_skip(0, banks[0][1], slice(2, PACK), 0, CHUNK)
-        store_round(0)
+        store(0)
+        round_out(nc.scalar.copy, 0, 0, CHUNK)
         banks.append(second_layer(2))
-        add_skip(1, banks[1][0], every_row, 0, CHUNK // 2)
+        add_and_round(1, 0, CHUNK // 2, nc.scalar.copy)
         banks.append(second_layer(LAST))
-        add_skip(1, banks[1][0], every_row, CHUNK // 2, CHUNK)
-        store_round(1)
+        add_and_round(1, CHUNK // 2, CHUNK, nc.scalar.copy)
+        store(1)
         for c in range(2, CHUNKS):
-            add_skip(c, banks[c][0], every_row, 0, CHUNK)
-            store_round(c)
+            add_and_round(c, 0, CHUNK // 2, nc.scalar.copy)
+            if c < LAST:
+                add_and_round(c, CHUNK // 2, CHUNK, nc.scalar.copy)
+            else:
+                add_skip(c, banks[c][0], slice(0, PACK), CHUNK // 2, CHUNK)
+                round_out(nc.scalar.copy, c, CHUNK // 2, 3 * CHUNK // 4)
+                round_out(nc.vector.tensor_copy, c, 3 * CHUNK // 4, CHUNK)
+            store(c)
         quantise_out(0, 2)
         quantise_out(2, LAST)
         quantise_out(LAST, CHUNKS)

from contextlib import ExitStack

import concourse.mybir as mybir

K, T, S, H, N = 512, 1024, 512, 512, 512
FLOPS = 2 * S * (2 * K * H + H * N)

F32 = mybir.dt.float32
BF16 = mybir.dt.bfloat16
I32 = mybir.dt.int32
U32 = mybir.dt.uint32
U16 = mybir.dt.uint16
U8 = mybir.dt.uint8
FP8X4 = mybir.dt.float8_e4m3fn_x4
FP4X4 = mybir.dt.float4_e2m1fn_x4
SILU = mybir.ActivationFunctionType.Silu
ADD = mybir.AluOpType.add

P = 128
PACK = 4
QUADRANT = 32
SCALE_ROWS = 16
CHUNK = 128
CHUNKS = S // CHUNK
LAST = CHUNKS - 1
LIST_COLS = CHUNK // 16
SKIP_SPLIT = CHUNK + CHUNK // 2
VECTOR_GROUPS = 50
HALF = H // 2
GROUPS = HALF // PACK
X_ROW = 4
E_ROW = 8


def tile_picked_zeagle_silu_po_kernel(
    tc, x_words, x_scales, e_words, e_scales, w1, w2, w3_words, w3_scales, skip, offs, tok,
    out_0, out_1, out_2,
):
    nc = tc.nc
    with ExitStack() as ctx:
        keep = ctx.enter_context(tc.tile_pool(name="keep", bufs=1))
        psum = ctx.enter_context(tc.psum_pool(name="psum", bufs=1))

        def tile(shape, dtype, name, tag=None):
            return keep.tile(shape, dtype, name=name, tag=tag or name, align_bytes=256)

        def columns(first, last):
            return slice(first * CHUNK, last * CHUNK)

        def entries(list_tile, first, last):
            return list_tile[:, first * LIST_COLS : last * LIST_COLS]

        def load_scale_rows(plane, rows, first_row=0):
            for r in range(PACK):
                nc.sync.dma_start(
                    out=plane[first_row + r : P : QUADRANT, :].bitcast(I32),
                    in_=rows[0, r:SCALE_ROWS:PACK, :].bitcast(I32),
                )

        def load_rows(matrix, cols, name):
            raw = tile([P, PACK, cols.stop - cols.start], F32, name)
            nc.sync.dma_start(out=raw[:], in_=matrix[:, cols].rearrange("(p j) c -> p j c", j=PACK))
            return raw

        def load_half(w, name, half):
            return load_rows(w, slice(half * HALF, (half + 1) * HALF), name + str(half))

        def load_words(words, name):
            table = tile([P, T], I32, name)
            nc.sync.dma_start(out=table[:], in_=words[0].rearrange("p c r -> p (c r)").bitcast(I32))
            return table

        offs_sb = tile([P, S // 16], U16, "offs_sb")
        tok_sb = tile([P, S // 16], U16, "tok_sb")
        xs_table = tile([P, T], U8, "xs_table")
        es_table = tile([P, T], U8, "es_table")
        w3s_raw = tile([P, N], U8, "w3s_raw")

        nc.vector.memset(xs_table[:].bitcast(I32), 0)
        for plane in (es_table, w3s_raw):
            nc.gpsimd.memset(plane[:].bitcast(I32), 0)

        warm_in = tile([P, 8], F32, "warm_in")
        warm_out = tile([P, 8], F32, "warm_out")
        nc.gpsimd.memset(warm_in[:], 0.0)
        nc.scalar.activation(out=warm_out[:], in_=warm_in[:], func=SILU)

        xw_table = load_words(x_words, "xw_table")
        nc.sync.dma_start(offs_sb[:], offs)
        w1_raw = [load_half(w1, "w1_raw", 0)]
        load_scale_rows(xs_table, x_scales, X_ROW)
        w1_raw.append(load_half(w1, "w1_raw", 1))
        w2_raw = [load_half(w2, "w2_raw", 0)]
        nc.sync.dma_start(tok_sb[:], tok)
        load_scale_rows(es_table, e_scales, E_ROW)
        w2_raw.append(load_half(w2, "w2_raw", 1))
        ew_table = load_words(e_words, "ew_table")
        w3w_raw = tile([P, 2 * N], U8, "w3w_raw")
        nc.sync.dma_start(out=w3w_raw[:].bitcast(I32), in_=w3_words[0].bitcast(I32))
        load_scale_rows(w3s_raw, w3_scales)
        skip_first = load_rows(skip, slice(0, SKIP_SPLIT), "skip_first")
        skip_rest = load_rows(skip, slice(SKIP_SPLIT, S), "skip_rest")

        def round_and_deal(copy, grouped, raw, half, first, last):
            g0 = half * GROUPS
            copy(
                out=grouped[:, :, g0 + first : g0 + last, :].rearrange("p (u v) g j -> p u g j v", v=2),
                in_=raw[half][:].rearrange("p j (g u v) -> p u g j v", u=2, v=2)[:, :, first:last, :, :],
            )

        def round_pair(copy, grouped, raw, u, first=0, last=GROUPS):
            copy(
                out=grouped[:, 2 * u : 2 * u + 2, GROUPS + first : GROUPS + last, :].rearrange("p v g j -> p g j v"),
                in_=raw[1][:].rearrange("p j (g t) -> p g j t", t=PACK)[:, first:last, :, 2 * u : 2 * u + 2],
            )

        def round_weight(grouped, raw):
            round_and_deal(nc.scalar.copy, grouped, raw, 0, 0, GROUPS)
            round_pair(nc.vector.tensor_copy, grouped, raw, 0, 0, VECTOR_GROUPS)
            round_pair(nc.scalar.copy, grouped, raw, 0, VECTOR_GROUPS, GROUPS)
            round_pair(nc.scalar.copy, grouped, raw, 1)

        def quantise_weight(codes, plane, grouped):
            for u in range(2):
                places = slice(2 * u * P, (2 * u + 2) * P)
                quantise(codes[:, places], plane[:, places], grouped[:, 2 * u : 2 * u + 2, :, :].rearrange("p t g j -> p (t g j)"))

        def quantise(codes, plane, values):
            nc.vector.quantize_mx(out=codes.bitcast(FP8X4), scales=plane, in_=values)

        xs_picked = tile([P, S], U8, "xs_picked")
        w1_grouped = tile([P, PACK, P, PACK], BF16, "w1_grouped")
        w2_grouped = tile([P, PACK, P, PACK], BF16, "w2_grouped")
        w1_codes = tile([P, H], U32, "w1_codes")
        w2_codes = tile([P, H], U32, "w2_codes")
        w2_plane = tile([P, H], U8, "w2_plane")
        w3_codes = tile([P, PACK, P, 2], U8, "w3_codes")

        xw_picked = tile([P, S], U32, "xw_picked")
        nc.vector.tensor_copy(xw_picked[:], xw_table[:].bitcast(U32).indirect(offs_sb[:]))
        nc.vector.tensor_copy(xs_picked[:], xs_table[:].indirect(offs_sb[:]))
        round_weight(w1_grouped, w1_raw)
        w1_plane = tile([P, H], U8, "w1_plane")
        quantise_weight(w1_codes, w1_plane, w1_grouped)
        es_early = tile([P, LAST * CHUNK], U8, "es_early", tag="w1_raw1")
        nc.vector.tensor_copy(es_early[:], es_table[:].indirect(entries(tok_sb, 0, LAST)))

        round_weight(w2_grouped, w2_raw)
        quantise_weight(w2_codes, w2_plane, w2_grouped)

        ew_picked = tile([P, S], U32, "ew_picked", tag="w2_raw1")

        def gather_e_words(first, last):
            nc.vector.tensor_copy(
                ew_picked[:, columns(first, last)],
                ew_table[:].bitcast(U32).indirect(entries(tok_sb, first, last)),
            )

        y_codes = tile([P, S], U32, "y_codes")
        y_plane = tile([P, S], U8, "y_plane")
        h_bf = [tile([P, CHUNK, PACK], BF16, "h_bf%d" % c) for c in range(CHUNKS)]
        y_bf = tile([P, S, PACK], BF16, "y_bf")
        y_f32 = [tile([P, PACK, CHUNK], F32, "y_f32%d" % c) for c in range(CHUNKS)]
        pre = [psum.tile([P, PACK, CHUNK], F32, name="pre%d" % c) for c in range(CHUNKS)]

        def x_pass(c, t):
            cols = columns(c, c + 1)
            places = slice(t * P, (t + 1) * P)
            nc.tensor.matmul_mx(
                out=pre[c][:, t, :], lhsT=w1_codes[:, places].bitcast(FP8X4), lhsT_scale=w1_plane[:, places],
                rhs=xw_picked[:, cols].bitcast(FP8X4), rhs_scale=xs_picked[X_ROW:P, cols],
                start=t == 0, stop=False,
            )

        def e_pass(c, t):
            cols = columns(c, c + 1)
            places = slice(t * P, (t + 1) * P)
            nc.tensor.matmul_mx(
                out=pre[c][:, t, :], lhsT=w2_codes[:, places].bitcast(FP8X4), lhsT_scale=w2_plane[:, places],
                rhs=ew_picked[:, cols].bitcast(FP8X4),
                rhs_scale=es_late[E_ROW:P, :] if c == LAST else es_early[E_ROW:P, cols],
                start=False, stop=t == PACK - 1,
            )

        def pieces(c):
            width = CHUNK // 2 if c == 0 else CHUNK
            return [slice(n, n + width) for n in range(0, CHUNK, width)]

        def first_layer(c):
            for t in range(PACK):
                e_pass(c, t)
            for part in pieces(c):
                nc.scalar.activation(
                    out=h_bf[c][:, part, :], in_=pre[c][:, :, part].rearrange("p t n -> p n t"), func=SILU
                )

        def second_layer(c):
            cols = columns(c, c + 1)
            h_codes = tile([P, CHUNK], U32, "h_codes%d" % c, tag="h_codes%d" % (c % 2))
            for part in pieces(c):
                place = slice(cols.start + part.start, cols.start + part.stop)
                quantise(h_codes[:, part], h_plane[:, place], h_bf[c][:, part, :].rearrange("p n t -> p (n t)"))
            if c == 0:
                parts = [
                    psum.tile([P, 2, CHUNK], F32, name="post%d" % c),
                    psum.tile([P, 2, CHUNK], F32, name="post%db" % c, tag="pre%d" % min(c, 1)),
                ]
            else:
                parts = [psum.tile([P, PACK, CHUNK], F32, name="post%d" % c)]
            width = PACK // len(parts)
            for t in range(PACK):
                nc.tensor.matmul_mx(
                    out=parts[t // width][:, t % width, :],
                    lhsT=w3_codes[:, t, :, :].rearrange("p g b -> p (g b)").bitcast(FP4X4),
                    lhsT_scale=w3_plane[:, t, :],
                    rhs=h_codes[:].bitcast(FP8X4), rhs_scale=h_plane[:, cols],
                    start=True, stop=True,
                )
            return parts

        def round_out(copy, c, first, last):
            copy(
                out=y_bf[:, c * CHUNK + first : c * CHUNK + last, :].rearrange("p (a i) t -> p a t i", i=4),
                in_=y_f32[c][:, :, first:last].rearrange("p t (a i) -> p a t i", i=4),
            )

        def add_skip(c, part, rows, first, last):
            start, stop = c * CHUNK + first, c * CHUNK + last
            if stop <= SKIP_SPLIT:
                added = skip_first[:, rows, start:stop]
            else:
                added = skip_rest[:, rows, start - SKIP_SPLIT : stop - SKIP_SPLIT]
            nc.vector.tensor_tensor(y_f32[c][:, rows, first:last], part[:, :, first:last], added, ADD)

        def store(c):
            cols = columns(c, c + 1)
            nc.sync.dma_start(out=out_0[:, cols].rearrange("(p t) j -> p t j", t=PACK), in_=y_f32[c][:])

        def add_and_round(c, first, last, copy):
            add_skip(c, banks[c][0], slice(0, PACK), first, last)
            round_out(copy, c, first, last)

        def quantise_out(first, last):
            cols = columns(first, last)
            quantise(y_codes[:, cols], y_plane[:, cols], y_bf[:, cols, :].rearrange("p n t -> p (n t)"))

        for u in range(2):
            for c in range(CHUNKS):
                x_pass(c, 2 * u)
                x_pass(c, 2 * u + 1)
        gather_e_words(0, 1)
        gather_e_words(1, 2)
        gather_e_words(2, CHUNKS)
        nc.scalar.copy(
            out=w3_codes[:].rearrange("p t g b -> p (t g b)").bitcast(U16).rearrange("p (t g) -> p t g", t=PACK),
            in_=w3w_raw[:].bitcast(U16).rearrange("p (g t) -> p t g", t=PACK),
        )
        es_late = tile([P, CHUNK], U8, "es_late", tag="w3w_raw")
        nc.vector.tensor_copy(es_late[:], es_table[:].indirect(entries(tok_sb, LAST, CHUNKS)))
        first_layer(0)
        w3_plane = tile([P, PACK, P], U8, "w3_plane")
        nc.gpsimd.tensor_copy(w3_plane[:], w3s_raw[:].rearrange("p (g t) -> p t g", t=PACK))
        h_plane = tile([P, S], U8, "h_plane")
        for c in range(1, CHUNKS):
            first_layer(c)
        banks = [second_layer(c) for c in range(2)]
        add_skip(0, banks[0][0], slice(0, 2), 0, CHUNK)
        add_skip(0, banks[0][1], slice(2, PACK), 0, CHUNK)
        store(0)
        round_out(nc.scalar.copy, 0, 0, CHUNK)
        banks.append(second_layer(2))
        add_and_round(1, 0, CHUNK // 2, nc.scalar.copy)
        banks.append(second_layer(LAST))
        add_and_round(1, CHUNK // 2, CHUNK, nc.scalar.copy)
        store(1)
        for c in range(2, CHUNKS):
            add_and_round(c, 0, CHUNK // 2, nc.scalar.copy)
            if c < LAST:
                add_and_round(c, CHUNK // 2, CHUNK, nc.scalar.copy)
            else:
                add_skip(c, banks[c][0], slice(0, PACK), CHUNK // 2, CHUNK)
                round_out(nc.scalar.copy, c, CHUNK // 2, 3 * CHUNK // 4)
                round_out(nc.vector.tensor_copy, c, 3 * CHUNK // 4, CHUNK)
            store(c)
        quantise_out(0, 2)
        quantise_out(2, LAST)
        quantise_out(LAST, CHUNKS)
        nc.sync.dma_start(out=out_1[0].rearrange("p c r -> p (c r)").bitcast(I32), in_=y_codes[:].bitcast(I32))
        for r in range(PACK):
            nc.scalar.dma_start(
                out=out_2[0, r:SCALE_ROWS:PACK, :].bitcast(I32),
                in_=y_plane[r:P:QUADRANT, :].bitcast(I32),
            )
